import numpy as np, ml_dtypes
CORES = [16,17,18,19,32,33,34,35]
N = 8
import mx_ref
BF = ml_dtypes.bfloat16
def gentries(a):
    return np.ascontiguousarray(a.reshape(8, 16, -1).transpose(0, 2, 1)).reshape(8, -1)
def gtable(e):
    e = np.asarray(e); return np.ascontiguousarray(e.reshape(8, -1, 16).transpose(0, 2, 1)).reshape(128, -1).astype(np.int32)
def gcols(t, e):
    v = np.concatenate([t.reshape(8, 16, -1, 4), np.zeros((8, 16, 1, 4), BF)], axis=2)
    return np.ascontiguousarray(np.stack([v[g][:, e[g]] for g in range(8)])).reshape(128, -1)
def tile(rs):
    return np.stack(rs, axis=2).reshape(128, -1).astype(BF)
def pick(q, e):
    c = np.concatenate([q[0].reshape(128, -1, 4), np.zeros((128, 1, 4), np.uint8)], axis=1); s = np.concatenate([q[1], np.ones((16, 1), np.uint8)], axis=1)
    return (np.ascontiguousarray(c[:, e].reshape(128, -1)), np.ascontiguousarray(s[:, e]))
def join(*qs):
    return (np.concatenate([q[0] for q in qs], axis=1), np.concatenate([q[1] for q in qs], axis=1))
def put(q, e, v):
    c, s = q[0].reshape(128, -1, 4).copy(), q[1].copy(); c[:, e] = v[0].reshape(128, -1, 4); s[:, e] = v[1]
    return (c.reshape(128, -1), s)
def pk(c, s):
    return (np.ascontiguousarray(c), mx_ref.live(s))
def emit(q):
    return q[0], q[1]
def packed(v, rng):
    q = [mx_ref.quantize(np.ascontiguousarray(v[r])) for r in range(N)]
    return np.stack([a for a, b in q]), np.stack([mx_ref.plane(b, rng) for a, b in q])
def values_of_codes():
    e, c = np.zeros((128, 128, 4), np.float32), np.zeros((128, 2, 4), np.uint8)
    e[np.arange(128), np.arange(128), 0] = 1
    c[:127, :, 0] = np.arange(256).reshape(2, 128).T[:127]
    return mx_ref.matmul(mx_ref.quantize(e.reshape(128, 512).astype(BF)), (c.reshape(128, 8), np.full((16, 2), 127, np.uint8))).T.reshape(-1).astype(np.float64)
CODE_VALUE, SCALE_VALUE = values_of_codes(), 2.0 ** (np.arange(256) - 127.0)
def decode(q):
    return (CODE_VALUE[q[0]].reshape(16, 8, -1, 4) * SCALE_VALUE[q[1]][:, None, :, None] + 0.0).reshape(128, -1).astype(np.float32)
def f(rng, *shape):
    return mx_ref.flush((rng.standard_normal(shape, dtype=np.float32) * np.exp2(rng.integers(-2, 3, shape[:-1] + (1,)))).astype(BF))
def wide(rng, *shape, cols=0):
    v = rng.standard_normal(shape, dtype=np.float32) * np.exp2(rng.integers(-12, 13, shape)).astype(np.float32)
    if cols: v *= np.repeat(np.exp2(rng.integers(-cols, cols + 1, shape[:-2] + (1, shape[-1] // 4))) * (rng.random(shape[:-2] + (1, shape[-1] // 4)) > 0.0625), 4, axis=-1).astype(np.float32)
    return mx_ref.flush(v.astype(BF))
C, F = 384, 288
MASK = [1, 2, 4]
def numbers_of(rng):
    return {"x": np.array(f(rng, N, 128, 4 * C)), "u": np.array(f(rng, N, 128, 512)), "v": np.array(f(rng, N, 128, 512))}
def stored(k, n):
    return {"dl": np.stack([gtable(k[r]) for r in range(N)]), "nl": np.stack([gtable(n[r]) for r in range(N)])}
def lists(rng):
    e = np.tile(np.arange(C), (N, 8, 1))
    k, e = rng.permuted(e, axis=2), rng.permuted(e, axis=2)
    n = np.empty_like(e)
    np.put_along_axis(n, e, e.reshape(N, 8, -1, 2)[..., ::-1].reshape(N, 8, C), axis=2)
    return k, n
def layers(rng, still=[]):
    w = np.array(f(rng, N, 128, 2048)).reshape(N, 8, 16, 4, 8, 16, 4)
    for i in still:
        w[:, :, i] = 0
        w[:, :, :, :, :, i] = 0
    return w
def weights(rng, w):
    c, s = packed(np.ascontiguousarray(w).reshape(N, 128, 2048), rng)
    return {"wc": c, "ws": s}
def setup_inputs(rng):
    return {**numbers_of(rng), **stored(*lists(rng)), **weights(rng, layers(rng))}
def setup_inputs_ties(rng):
    d = numbers_of(rng)
    k, n = lists(rng)
    o, h = rng.permutation(N), rng.permutation(8)
    i = np.arange(N)
    e = (i ^ (i >> 1) ^ (i >> 2)) % 2
    s = rng.integers(0, 4, (N, 8, C))
    s[o[1]] += 1
    s[:, h[:3]] = 1
    for g in h[:2]:
        for r in np.flatnonzero(e):
            k[r, g] = n[r, g]
            s[r, g] = np.where(np.arange(C) < n[r, g], 2, 0)
    c = np.ones((N, 8), np.float32)
    c[o[0]] = 0
    c[o[1]] = -1
    c[:, h[:3]] = 1
    x = d["x"].reshape(N, 8, 16, C, 4)
    x[:, :, 0] = 0
    x[:, :, 0, :, 0] = s.astype(np.float32).astype(BF)
    a = np.exp2(rng.integers(-3, 4, (1, 8, 1)).astype(np.float32))
    x[:, :, 8:] = 0
    x[:, :, 8, :, 0] = (-1.125 * a).astype(BF)
    x[:, :, 10, :, 0] = (-0.0703125 * a).astype(BF)
    u = d["u"].reshape(N, 128, 128, 4)
    u[:, :, ::16] = 0
    w = layers(rng, [0])
    w[:, :, :, :, :, 8:] = 0
    for g in range(8):
        u[:, 16 * g, 16 * g, 0] = c[:, g].astype(BF)
        w[:, g, 8, 0, g, 8, 0] = -28.0
        for b in range(4): w[:, g, 10, b, g, 9, 0] = -2.0 ** (b - 5)
    return {"x": x.reshape(N, 128, 4 * C), "u": u.reshape(N, 128, 512), "v": d["v"], **stored(k, n), **weights(rng, w)}
def setup_inputs_near(rng):
    d = numbers_of(rng)
    k, n = lists(rng)
    x = d["x"].astype(np.float32).reshape(N, 8, 16, C, 4)
    x[:, :, 0] = 0
    x[:, :, 8:] = 0
    u = d["u"].reshape(N, 128, 128, 4)
    u[:, :, ::16] = 0
    w = layers(rng, [0, 8, 9, 10, 11, 12, 13, 14, 15])
    at = [0, C - 1, int(rng.integers(C)), int(rng.integers(C))]
    for i, g in enumerate(rng.permutation(8)):
        h, c = 16 * g, 1.0 if i < 2 else 2.0 ** -30
        s = rng.integers(0, 16, (N, C))
        digits = ((s[:, :, None] >> np.arange(4)) & 1) * np.exp2(np.arange(4) - 23.0)
        u[:, h, h, 0] = c
        if i < 4:
            x[:, g, 0, :, 0] = i % 2 * 3.0 - 1.5
            x[:, g, 8] = digits
            x[:, g, 11, :, 0] = 2.0 ** -10
            u[:, h + 11, h, 0] = c
        elif i < 6: x[:, g, 8] = digits * rng.choice([-1.0, 1.0], (N, C, 1))
        else:
            x[:, g, 10, :, 0] = rng.choice([-1.0, 1.0], (N, C)) * 2.0 ** -30
            x[:, g, 11, :, 0] = 2.0 ** -29
            w[:, g, 10, 0, g, 9, 0] = 2.0 ** -9
            w[:, g, 12, 0, g, 9, 0] = 1.0
            w[:, g, 10, 0, g, 13, 0] = -2.0 ** -9
            w[:, g, 12, 0, g, 13, 0] = 1.0
            w[:, g, 11, 0, g, 11, 0] = 16.0
            u[:, h + 9, h, 0] = 1.125 * c
            u[:, h + 13, h, 0] = c
        if i < 6: u[:, h + 8, h] = c
        if i % 2: x[:, g, 0, at[i // 2], 0] = 2.0 ** 29 * rng.choice([-1.0, 1.0], N)
    return {"x": x.reshape(N, 128, 4 * C).astype(BF), "u": u.reshape(N, 128, 512), "v": d["v"], **stored(k, n), **weights(rng, w)}
def setup_inputs_odd(rng):
    d = numbers_of(rng)
    x = (1.0 + (2 * rng.integers(0, 64, (N, 16, 8, C, 4)) + 1) * 2.0 ** -7) * np.exp2(-rng.integers(0, 7, (N, 16, 8, C, 4)).astype(np.float64)) * rng.choice([-1.0, 1.0], (N, 16, 8, C, 4))
    x[:, :, 0, :, 0] = 1.96875 * 2.0 ** 8 * rng.choice([-1.0, 1.0], (N, 16, C))
    x[:, ::2, 1, :, 0] = (8 + rng.integers(0, 2, (N, 8, C))) * 2.0 ** -8
    u = d["u"].reshape(N, 128, 128, 4)
    u[:, :, ::16] = 0
    for h in range(0, 128, 16): u[:, h + 1, h, 0] = 1.0
    return {"x": x.astype(np.float32).reshape(N, 128, 4 * C).astype(BF), "u": u.reshape(N, 128, 512), "v": d["v"], **stored(*lists(rng)), **weights(rng, layers(rng, [0, 8]))}
def setup_inputs_ends(rng):
    d = numbers_of(rng)
    k, n = lists(rng)
    j = np.arange(C)
    o = np.zeros(N, np.int64)
    for i, r in enumerate(rng.permutation([r for r in range(N) if not r & MASK[0]])):
        o[r], o[r ^ MASK[0]] = rng.permutation([1, 2] if i % 2 else [0, 3])
    e, h = rng.permutation(N) % 4, rng.permutation(N) % 4
    k[e == 0] = j
    k[e == 1] = j[::-1]
    k[e == 2] = (j + 1) % C
    n[h == 0] = j[::-1]
    n[h == 1] = j ^ 1
    n[h == 2] = (j + C // 2) % C
    s = rng.choice([-1.0, 1.0], (N, 8, 16, C, 4))
    s[o == 0] = -1
    s[o == 1] = rng.choice([-1.0, 1.0], (N, 1, 1, C, 1))[o == 1]
    x = s * (0.955 + 0.02 * rng.random((N, 8, 16, C, 4))) * 2.0 ** 30
    x[o == 3] = 2.0 ** -30
    g = int(rng.integers(8))
    x[:, g, :8] = 2.0 ** -30
    size = np.where(o == 3, 2.0 ** -30, 2.0 ** 30)
    a = np.stack([rng.permutation(8) % 2 * 2.0 - 1.0 for r in range(N)]) * size[:, None]
    u = d["u"].reshape(N, 128, 128, 4)
    u[:, :, ::16] = a.astype(np.float32).astype(BF)[:, None, :, None]
    v = rng.choice([-1.0, 1.0], (N, 128, 512)) * size[:, None, None]
    w = np.zeros((N, 128, 4, 128, 4), np.float32)
    i, l = np.arange(128), np.arange(16 * g, 16 * g + 8)
    for b in range(4):
        w[:, i, b, i, b] = np.where(o == 3, 32.0, -0.125)[:, None]
        w[:, l, b, l, b] = np.where(o == 3, 256.0, 0.0)[:, None]
    return {"x": x.astype(np.float32).reshape(N, 128, 4 * C).astype(BF), "u": u.reshape(N, 128, 512), "v": v.astype(np.float32).astype(BF), **stored(k, n), **weights(rng, w.astype(BF))}
def setup_inputs_spread(rng):
    d = setup_inputs(rng)
    d["x"] = wide(rng, N, 128, 4 * C, cols=6)
    return d
def check_inputs(d):
    b = []
    for k in ("x", "u", "v"):
        a = np.abs(d[k].astype(np.float32))
        if not (np.isfinite(a).all() and ((a == 0) | (a >= 2.0 ** -30) & (a <= 2.0 ** 30)).all()): b.append("a value of " + k)
    none, least, most = [emit(mx_ref.quantize(np.full((128, 16), k, np.float32).astype(BF)))[1][0, 0] for k in (0.0, 2.0 ** -8, 2.0 ** 8)]
    top = emit(mx_ref.quantize(np.ascontiguousarray(np.tile(np.repeat(1.0 + np.arange(128) * 2.0 ** -7, 4), (128, 1))).astype(np.float32).astype(BF)))[0] & 0x7F
    for r in range(N):
        k, n = gentries(d["dl"][r]), gentries(d["nl"][r])
        if not (np.sort(k, axis=1) == np.arange(C)).all(): b.append("dl: not every column once")
        if not ((n >= 0) & (n < C)).all(): b.append("an entry of nl")
        elif not ((at(n, n) == np.arange(C)) & (n != np.arange(C))).all(): b.append("nl: not in pairs")
        if ((d["wc"][r] == 0x7F) | (d["wc"][r] == 0xFF)).any(): b.append("wc: a code that is no number")
        s = mx_ref.live(d["ws"][r])
        if ((s != none) & ((s < least) | (s > most))).any(): b.append("ws: a scale out of range")
        a = np.max(d["wc"][r].reshape(16, 8, 512, 4) & 0x7F, axis=(1, 3))
        if ((s == none) & (a != 0)).any(): b.append("wc: a code other than zero under the scale of zeros")
        if ((s != none) & ((a < top.min()) | (a > top.max()))).any(): b.append("wc: a block whose largest code isn't one of quantize_mx")
    return b
def at(t, e):
    return np.take_along_axis(t, e, axis=1)
def layer(w, q):
    return tile([mx_ref.matmul(pick(w, np.arange(128 * b, 128 * b + 128)), q) * np.float32(0.03125) for b in range(4)])
def reference(x, u, v, dl, nl, wc, ws):
    qu = [mx_ref.quantize(u[r]) for r in range(N)]
    lay = [pk(wc[r], ws[r]) for r in range(N)]
    d, n = [gentries(dl[r]) for r in range(N)], [gentries(nl[r]) for r in range(N)]
    now = [x[r] for r in range(N)]
    for m in MASK:
        s = [mx_ref.matmul(qu[r], mx_ref.quantize(now[r]))[::16] + np.float32(0.0) for r in range(N)]
        new, h, made = [], [], []
        for r in range(N):
            p = r ^ m
            a, b, k = np.tile(np.arange(C), (8, 1)), n[r], np.zeros((8, C), np.int64)
            for step in range(6):
                own = at(s[r], a) > at(s[p], b)
                a, b, k = np.where(own, at(d[r], a), a), np.where(own, b, at(d[p], b)), k + own
            z = ((gcols(now[r], a).astype(np.float32) + gcols(now[r], b).astype(np.float32)) * np.float32(0.5)).astype(BF)
            h.append(layer(lay[r], mx_ref.quantize(z)))
            new.append(np.where((k + at(k, n[r])) % 2 == 1, at(d[r], n[r]), d[r]))
        for r in range(N):
            p = r ^ m
            far = decode(mx_ref.quantize(np.ascontiguousarray(h[p][:, :4 * F]))).astype(BF)
            both = np.concatenate([far, h[r][:, 4 * F:]], axis=1)
            place = at(np.argsort(d[p], axis=1), new[r])
            made.append((now[r].astype(np.float32) + gcols(both, place).astype(np.float32)).astype(BF))
        now, d = made, new
    y, dn = np.zeros((N, 128, C), np.float32), np.zeros((N, 8, C), np.float32)
    oc, osc = np.zeros((N, 128, 4 * C), np.uint8), np.zeros((N, 16, C), np.uint8)
    for r in range(N):
        q = mx_ref.quantize(now[r])
        y[r] = mx_ref.matmul(mx_ref.quantize(v[r]), q)
        dn[r] = d[r]
        oc[r], osc[r] = emit(q)
    return {"y": y, "dn": dn, "oc": oc, "osc": osc}

@@ -1,0 +1,558 @@
+from concourse.mybir import AluOpType as A, ActivationFunctionType as F, dt
+
+C, FAR, NR = 384, 288, 3
+MASKS = [1, 2, 4]
+ZP = [(0, 160), (160, 384)]
+HP = [(0, 160), (160, 288)]
+SP = [(0, 192), (192, 384)]
+HUGE = 1e29
+ONE = 2.0 ** 80
+MAGIC = 1.5 * 2.0 ** 23
+L1, L2, L3 = {1, 3, 4, 6}, {2, 3, 5, 6}, {4, 5, 6}
+
+SCRATCH = {
+    "x0": ("sbuf", [128, 4 * C], "bfloat16"),
+    "xa1": ("sbuf", [128, 4 * C], "bfloat16"),
+    "xa2": ("sbuf", [128, 4 * C], "bfloat16"),
+    "xa3": ("sbuf", [128, 4 * C], "bfloat16"),
+    "hx": ("sbuf", [128, 4 * C], "bfloat16"),
+    "za": ("sbuf", [128, 4 * C], "bfloat16"),
+    "zt": ("sbuf", [128, 4 * C], "bfloat16"),
+    "ht": ("sbuf", [128, 4 * FAR], "bfloat16"),
+    "jt": ("sbuf", [128, 4 * C], "bfloat16"),
+    "u0": ("sbuf", [128, 512], "bfloat16"),
+    "v0": ("sbuf", [128, 512], "bfloat16"),
+    "ones": ("sbuf", [128, 512], "bfloat16"),
+    "eb": ("sbuf", [128, 2048], "bfloat16"),
+    "kp": ("sbuf", [128, 24, 16], "bfloat16"),
+    "rk": ("sbuf", [128, 416], "bfloat16"),
+    "qk": ("sbuf", [128, 26, 16], "bfloat16"),
+    "pb": ("psum", [128, 4096], "float32"),
+    "dli": ("sbuf", [128, 24], "int32"),
+    "nli": ("sbuf", [128, 24], "int32"),
+    "ia": ("sbuf", [128, 24], "int32"),
+    "ib": ("sbuf", [128, 24], "int32"),
+    "ic": ("sbuf", [128, 24], "int32"),
+    "im": ("sbuf", [128, 72], "int32"),
+    "iu": ("sbuf", [128, 8], "int32"),
+    "ij": ("sbuf", [128, 24], "int32"),
+    "ik": ("sbuf", [128, 24], "int32"),
+    "kk": ("sbuf", [128, 24], "int32"),
+    "kf": ("sbuf", [128, 24], "int32"),
+    "lu": ("sbuf", [128, 8], "uint16"),
+    "lrho": ("sbuf", [128, 48], "uint16"),
+    "lrho2": ("sbuf", [128, 24], "uint16"),
+    "ln": ("sbuf", [128, 24], "uint16"),
+    "lnr": ("sbuf", [128, 24], "uint16"),
+    "la": ("sbuf", [128, 24], "uint16"),
+    "lb": ("sbuf", [128, 24], "uint16"),
+    "ll": ("sbuf", [128, 24], "uint16"),
+    "vt": ("sbuf", [128, 22, 16], "float32"),
+    "ct": ("sbuf", [128, 352], "float32"),
+    "kt": ("sbuf", [128, 24, 16], "float32"),
+    "ps3": ("sbuf", [128, 24, 16], "float32"),
+    "po3": ("sbuf", [128, 24, 16], "float32"),
+    "pt3": ("sbuf", [128, 24, 16], "float32"),
+    "c6": ("sbuf", [128, 24, 6], "float32"),
+    "m6": ("sbuf", [128, 48, 6], "float32"),
+    "m3": ("sbuf", [128, 48, 3], "float32"),
+    "m1": ("sbuf", [128, 48], "float32"),
+    "m2": ("sbuf", [128, 48], "float32"),
+    "m0": ("sbuf", [128, 48], "float32"),
+    "tk": ("sbuf", [128, 48], "float32"),
+    "ab": ("sbuf", [128, 24, 3], "float32"),
+    "ai": ("sbuf", [128, 72], "float32"),
+    "oab": ("sbuf", [128, 72], "float32"),
+    "base": ("sbuf", [128, 48], "float32"),
+    "mo": ("sbuf", [128, 72], "float32"),
+    "mi": ("sbuf", [128, 72], "float32"),
+    "iota": ("sbuf", [128, C], "float32"),
+    "tw0": ("sbuf", [128, C], "float32"),
+    "wo0": ("sbuf", [128, C], "float32"),
+    "wo1": ("sbuf", [128, C], "float32"),
+    "fo": ("sbuf", [128, C], "float32"),
+    "wt0": ("sbuf", [128, C], "float32"),
+    "wt1": ("sbuf", [128, C], "float32"),
+    "ft": ("sbuf", [128, C], "float32"),
+    "vv": ("sbuf", [128, C], "float32"),
+    "einv": ("sbuf", [128, C], "float32"),
+    "knr": ("sbuf", [128, C], "float32"),
+    "kno": ("sbuf", [128, 24], "float32"),
+    "lr": ("sbuf", [128, C], "float32"),
+    "lr2": ("sbuf", [128, C], "float32"),
+    "lo": ("sbuf", [128, 24], "float32"),
+    "rt": ("sbuf", [128, 3 * C], "float32"),
+    "rq": ("sbuf", [128, 2 * C], "float32"),
+    "rqd": ("sbuf", [128, C], "float32"),
+    "od23": ("sbuf", [128, 48], "float32"),
+    "dno": ("sbuf", [128, 24], "float32"),
+    "dd": ("sbuf", [128, 24], "float32"),
+    "fd": ("sbuf", [128, 24], "float32"),
+    "ff": ("sbuf", [128, 24], "float32"),
+    "fg": ("sbuf", [128, 24], "float32"),
+    "ysb": ("sbuf", [128, C], "float32"),
+    "uq": ("sbuf", [128, 128], "float8_e4m3fn_x4"), "uqs": ("sbuf", [128, 128], "uint8"),
+    "ur": ("sbuf", [128, 128], "float8_e4m3fn_x4"), "urs": ("sbuf", [128, 128], "uint8"),
+    "vq": ("sbuf", [128, 128], "float8_e4m3fn_x4"), "vqs": ("sbuf", [128, 128], "uint8"),
+    "wq": ("sbuf", [128, 512], "float8_e4m3fn_x4"), "wqs": ("sbuf", [128, 512], "uint8"),
+    "eq": ("sbuf", [128, 512], "float8_e4m3fn_x4"), "eqs": ("sbuf", [128, 512], "uint8"),
+    "xq": ("sbuf", [128, C], "float8_e4m3fn_x4"), "xqs": ("sbuf", [128, C], "uint8"),
+    "zq": ("sbuf", [128, C], "float8_e4m3fn_x4"), "zqs": ("sbuf", [128, C], "uint8"),
+}
+SEMAPHORES = ["cv", "cs", "ct", "cg", "loc", "out"]
+LOADS = ["x", "u", "v", "wc", "wsp", "dl", "nl"]
+SEMAPHORES += ["ld_" + k for k in LOADS] + ["d_n"]
+for _r in range(NR):
+    SCRATCH["sc%d" % _r] = ("sbuf", [128, 24], "float32")
+    SCRATCH["tc%d" % _r] = ("sbuf", [128, 24], "float32")
+    SCRATCH["ld%d" % _r] = ("sbuf", [128, 24], "uint16")
+    SCRATCH["lp%d" % _r] = ("sbuf", [128, 48], "uint16")
+    SCRATCH["le%d" % _r] = ("sbuf", [128, 24], "uint16")
+    SCRATCH["lg%d" % _r] = ("sbuf", [128, 48], "uint16")
+    for _k in ("hq", "hl"):
+        SCRATCH["%s%d" % (_k, _r)] = ("sbuf", [128, FAR], "float8_e4m3fn_x4")
+        SCRATCH["%ss%d" % (_k, _r)] = ("sbuf", [128, FAR], "uint8")
+    SEMAPHORES += [k + str(_r) for k in ("a_sc", "a_le", "a_lg", "d_p2_", "d_p3_", "d_dn", "d_kn", "d_l")]
+    SEMAPHORES += ["a_h%d_%d" % (_r, p) for p in range(len(HP))]
+SCRATCH["ldf"] = ("sbuf", [128, 24], "uint16")
+
+
+def rank_program(g, core, T, topo):
+    rank = T.rank_of(core)
+    if rank is None:
+        return
+    que = {"v": g.vector, "s": g.scalar, "t": g.tensor, "g": g, "y": g.sync}
+    total, know, recs = {}, {}, {}
+    clk = {e: {} for e in que}
+
+    def need(e, ev):
+        sem, val = ev
+        c = clk[e]
+        if c.get(sem, 0) >= val:
+            return
+        que[e].wait_ge(T.sem[sem], val)
+        c[sem] = val
+        for k, w in know.get(ev, {}).items():
+            if c.get(k, 0) < w:
+                c[k] = w
+
+    def reg(r):
+        r = (r,) if isinstance(r, str) else r
+        return (r[0], r[1] if len(r) > 1 else 0, r[2] if len(r) > 2 else 1 << 30, r[3] if len(r) > 3 else None)
+
+    def hazards(e, rd, wr):
+        evs = []
+        for w, regs in ((False, rd), (True, wr)):
+            for r in regs:
+                n, lo, hi, ph = reg(r)
+                for (l2, h2, p2, w2, ev, e2) in recs.get(n, ()):
+                    if l2 < hi and lo < h2 and (ph is None or p2 is None or ph == p2) and (w or w2 or (n == "pb" and e2 != e)):
+                        evs.append(ev)
+        best = {}
+        for s, v in evs:
+            best[s] = max(best.get(s, 0), v)
+        for s in sorted(best, key=lambda k: -best[k]):
+            need(e, (s, best[s]))
+
+    def note(e, rd, wr, ev):
+        for r in wr:
+            n, lo, hi, ph = reg(r)
+            recs[n] = [x for x in recs.get(n, []) if not (lo <= x[0] and x[1] <= hi and (ph is None or x[2] == ph))]
+            recs[n].append((lo, hi, ph, True, ev, e))
+        for r in rd:
+            n, lo, hi, ph = reg(r)
+            recs[n] = [x for x in recs.get(n, []) if x[3] or x[5] != e or x[:3] != (lo, hi, ph) or x[4][0] != ev[0]]
+            recs[n].append((lo, hi, ph, False, ev, e))
+
+    def op(e, fn, rd, wr):
+        hazards(e, rd, wr)
+        sem = "c" + e
+        total[sem] = total.get(sem, 0) + 1
+        ev = (sem, total[sem])
+        know[ev] = dict(clk[e])
+        fn(que[e]).then_inc(T.sem[sem], 1)
+        note(e, rd, wr, ev)
+
+    def dma(e, sem, out, in_, rd, wr):
+        hazards(e, rd, wr)
+        total[sem] = total.get(sem, 0) + 16
+        ev = (sem, total[sem])
+        know[ev] = dict(clk[e])
+        que[e].dma_start(out, in_).then_inc(T.sem[sem], 16)
+        note(e, rd, wr, ev)
+
+    def send(dst, sem, out, in_, rd):
+        hazards("g", rd, [])
+        rid, pid, _ = topo.addr(dst)
+        g.remote_dma(out, in_, T.sem[sem], T.sem["loc"], pid, rid, topo.mask(core, dst))
+        total["loc"] = total.get("loc", 0) + len(topo.engines(core, dst))
+
+    def lands(src, sem, times, names):
+        total[sem] = times * len(topo.engines(src, core))
+        for n in names:
+            recs.setdefault(n, []).append((n_lo(n), n_hi(n), None, True, (sem, total[sem]), "remote") if isinstance(n, str) else None)
+
+    def n_lo(n):
+        return 0
+
+    def n_hi(n):
+        return 1 << 30
+
+    def land_cols(src, sem, times, regs):
+        total[sem] = times * len(topo.engines(src, core))
+        for r in regs:
+            n, lo, hi, ph = reg(r)
+            recs.setdefault(n, []).append((lo, hi, None, True, (sem, total[sem]), "remote"))
+
+    part = [T.cores[rank ^ m] for m in MASKS]
+    for r in range(NR):
+        p = part[r]
+        land_cols(p, "a_sc%d" % r, 1, ["tc%d" % r])
+        land_cols(p, "a_le%d" % r, 1, ["le%d" % r])
+        land_cols(p, "a_lg%d" % r, 1, ["lg%d" % r])
+        for i, (a, b) in enumerate(HP):
+            land_cols(p, "a_h%d_%d" % (r, i), 2, [("hl%d" % r, a, b), ("hls%d" % r, a, b)])
+
+    def vts(out, in0, s1, s2, o0, o1, rd, wr):
+        if o1 is None:
+            op("v", lambda q: q.tensor_scalar(out, in0, s1, None, o0), rd, wr)
+        else:
+            op("v", lambda q: q.tensor_scalar(out, in0, s1, s2, o0, o1), rd, wr)
+
+    def vtt(out, a, b, o, rd, wr):
+        op("v", lambda q: q.tensor_tensor(out, a, b, o), rd, wr)
+
+    def vcp(out, in_, rd, wr):
+        op("v", lambda q: q.tensor_copy(out, in_), rd, wr)
+
+    def vms(ap, c, wr):
+        op("v", lambda q: q.memset(ap, c), [], wr)
+
+    def vtr(out, in_, rd, wr):
+        op("v", lambda q: q.transpose(out, in_), rd, wr)
+
+    def act(out, in_, rd, wr, scale=None, bias=None):
+        if bias is not None:
+            op("s", lambda q: q.activation(out, in_, F.Identity, bias=bias, scale=1.0 if scale is None else scale), rd, wr)
+        elif scale is not None:
+            op("s", lambda q: q.activation(out, in_, F.Copy, scale=scale), rd, wr)
+        else:
+            op("s", lambda q: q.activation(out, in_, F.Copy), rd, wr)
+
+    def quant(q_, s_, in_, rd, wr):
+        op("v", lambda q: q.quantize_mx(q_, s_, in_), rd, wr)
+
+    def mm(bank, w, l, ls, r_, rs, rd):
+        op("t", lambda q: q.matmul_mx(T.pb[:, 512 * bank:512 * bank + w], l, ls, r_, rs, True, True), rd, [("pb", bank, bank + 1)])
+
+    def cc(k):
+        return T.ct[:, 32 * k:32 * k + 1]
+
+    dma("y", "ld_dl", T.dli[:], T.dl[:], [], ["dli"])
+    dma("s", "ld_u", T.u0[:], T.u[:], [], ["u0"])
+    dma("y", "ld_x", T.x0[:], T.x[:], [], ["x0"])
+    dma("s", "ld_nl", T.nli[:], T.nl[:], [], ["nli"])
+    dma("y", "ld_wc", T.wq[:].bitcast(dt.uint8), T.wc[:], [], ["wq"])
+    dma("y", "ld_wsp", T.wqs[:], T.ws[:], [], ["wqs"])
+    dma("y", "ld_v", T.v0[:], T.v[:], [], ["v0"])
+
+    def iota(name, pattern, cm, fl=False):
+        if fl:
+            op("g", lambda q: q.iota(T[name][:], pattern, 0, cm, allow_small_or_imprecise_dtypes=True), [], [name])
+        else:
+            op("g", lambda q: q.iota(T[name][:], pattern, 0, cm), [], [name])
+
+    iota("iota", [[1, C]], 0, True)
+    iota("iu", [[16, 8]], 0)
+    iota("ia", [[16, 24]], 0)
+    iota("ib", [[0, 24]], 1)
+    iota("ic", [[32, 12], [0, 2]], 0)
+    iota("im", [[16, 24], [0, 3]], 1)
+
+    own_q = [q if q < 6 else None for q in range(8)] + [q if q < 7 else None for q in range(8)]
+    far_q = [5 - q if q < 6 else None for q in range(8)] + [6 - q if q < 7 else None for q in range(8)]
+
+    def bias(qs, lv):
+        return [HUGE if q is None or q not in lv else (0.0 if r < 8 else -1024.0 * ONE) for r, q in enumerate(qs)]
+
+    def dec(qs):
+        return [0.0 if r < 8 else (1024.0 * sum(q in lv for lv in (L1, L2, L3)) if q is not None else 0.0) - 4096.0 + 1024.0 * (r - 7) - 192.0 for r, q in enumerate(qs)]
+
+    cols = [bias(own_q, L1), bias(own_q, L2), bias(own_q, L3), bias(far_q, L1), bias(far_q, L2), bias(far_q, L3),
+            [1.0] * 8 + [1.0 / ONE] * 8, dec(own_q), dec(far_q), [0.0] * 8 + [ONE] * 8, [-HUGE] * 8 + [4096.0 * ONE] * 8]
+
+    def d_lists(r):
+        return T["ld%d" % r][:] if r < NR else T.ldf[:]
+
+    def first_list():
+        vcp(T["ld0"][:], T.dli[:], ["dli"], ["ld0"])
+
+    vms(T.vt[:], HUGE, ["vt"])
+    for k, vals in enumerate(cols):
+        r0 = 0
+        if k == 4:
+            first_list()
+        while r0 < 16:
+            r1 = r0
+            while r1 < 16 and vals[r1] == vals[r0]:
+                r1 += 1
+            if vals[r0] != HUGE:
+                a0, a1, val = r0, r1, float(vals[r0])
+                vms(T.vt[:, 2 * k:2 * k + 2, a0:a1], val, [("vt", 32 * k, 32 * k + 32, (k, r0))])
+            r0 = r1
+    vtr(T.ct[:], T.vt[:], ["vt"], ["ct"])
+    vts(T.tw0[:], T.iota[:], cc(9), cc(10), A.mult, A.add, ["iota", "ct"], ["tw0"])
+    vcp(T.fd[:], T.dli[:], ["dli"], ["fd"])
+    vcp(T.lu[:], T.iu[:], ["iu"], ["lu"])
+    vcp(T.ln[:], T.nli[:], ["nli"], ["ln"])
+    vts(T.ij[:], T.ib[:], 15, None, A.bitwise_and, None, ["ib"], ["ij"])
+    vtt(T.ij[:], T.ij[:], T.ia[:], A.add, ["ij", "ia"], ["ij"])
+
+    def rho(dst_f):
+        vts(T.ff[:], T.ij[:], 1.0 / 24.0, -11.5 / 24.0, A.mult, A.add, ["ij"], ["ff"])
+        vcp(T.ik[:], T.ff[:], ["ff"], ["ik"])
+        vts(T.ff[:], T.ik[:], -383.0, None, A.mult, None, ["ik"], ["ff"])
+        vts(T.fg[:], T.ij[:], 16.0, None, A.mult, None, ["ij"], ["fg"])
+        vtt(T.ij[:], T.ff[:], T.fg[:], A.add, ["ff", "fg"], ["ij"])
+
+    rho(None)
+    vcp(T.lrho[:, 0:24], T.ij[:], ["ij"], [("lrho", 0, 24)])
+    vts(T.lrho[:, 24:48], T.ij[:], 384.0, None, A.add, None, ["ij"], [("lrho", 24, 48)])
+    rho(None)
+    vcp(T.lrho2[:], T.ij[:], ["ij"], ["lrho2"])
+
+    def power1(r):
+        ld = T["ld%d" % r][:]
+        act(T.rt[:, 0:C], T.iota[:].indirect(ld), ["iota", "ld%d" % r], [("rt", 0, C)])
+
+    def powers2(r):
+        ld = T["ld%d" % r][:]
+        act(T.rt[:, C:2 * C], T.rt[:, 0:C].indirect(ld), [("rt", 0, C), "ld%d" % r], [("rt", C, 2 * C)])
+        act(T.rt[:, 2 * C:3 * C], T.rt[:, C:2 * C].indirect(ld), [("rt", C, 2 * C), "ld%d" % r], [("rt", 2 * C, 3 * C)])
+        act(T.rq[:], T.rt[:, C:3 * C].indirect(T.lrho[:]), [("rt", C, 3 * C), "lrho"], ["rq"])
+        dma("y", "d_p2_%d" % r, T.od23[:, 0:24], T.rq[0:128:16, 0:C], ["rq"], [("od23", 0, 24)])
+        dma("y", "d_p3_%d" % r, T.od23[:, 24:48], T.rq[0:128:16, C:2 * C], ["rq"], [("od23", 24, 48)])
+
+    def mates_list(r):
+        act(T.rqd[:], T.rt[:, 0:C].indirect(T.lnr[:]), [("rt", 0, C), "lnr"], ["rqd"])
+        dma("y", "d_dn%d" % r, T.dno[:], T.rqd[0:128:16, :], ["rqd"], ["dno"])
+
+    def send_d(r):
+        send(part[r], "a_le%d" % r, T["le%d" % r][:], T["ld%d" % r][:], ["ld%d" % r])
+
+    def send_powers(r):
+        vcp(T["lp%d" % r][:], T.od23[:], ["od23"], ["lp%d" % r])
+        send(part[r], "a_lg%d" % r, T["lg%d" % r][:], T["lp%d" % r][:], ["lp%d" % r])
+
+    send_d(0)
+    power1(0)
+    powers2(0)
+
+    quant(T.uq[:], T.uqs[:], T.u0[:], ["u0"], ["uq", "uqs"])
+    vcp(T.ur[:].bitcast(dt.uint32), T.uq[:].bitcast(dt.uint32).indirect(T.lu[:]), ["uq", "lu"], ["ur"])
+    vcp(T.urs[:], T.uqs[:].indirect(T.lu[:]), ["uqs", "lu"], ["urs"])
+
+    def score(xn, i):
+        a, b = SP[i]
+        quant(T.xq[:, a:b], T.xqs[:, a:b], T[xn][:, 4 * a:4 * b], [(xn, 4 * a, 4 * b)], [("xq", a, b), ("xqs", a, b)])
+        mm(i, b - a, T.ur[:], T.urs[:], T.xq[:, a:b], T.xqs[:, a:b], ["ur", "urs", ("xq", a, b), ("xqs", a, b)])
+
+    score("x0", 0)
+    score("x0", 1)
+
+    def rest_of_constants():
+        vts(T.ij[:], T.ib[:], 31, None, A.bitwise_and, None, ["ib"], ["ij"])
+        vtt(T.ff[:], T.ij[:], T.ic[:], A.add, ["ij", "ic"], ["ff"])
+        for i in range(8, 16):
+            vts(T.kt[:, :, i], T.ff[:], 4096.0, ONE, A.add, A.mult, ["ff"], [("kt", 0, 384, i)])
+        vms(T.kt[:, :, 6:8], 0.0, [("kt", 0, 384, 6)])
+        vts(T.im[:], T.im[:], 4, 1, A.logical_shift_right, A.bitwise_and, ["im"], ["im"])
+        vcp(T.mo[:], T.im[:], ["im"], ["mo"])
+        vts(T.mi[:], T.mo[:], -1.0, 1.0, A.mult, A.add, ["mo"], ["mi"])
+        vms(T.kp[:], 0.0, ["kp"])
+        vms(T.rk[:], 0.0, ["rk"])
+        vms(T.ones[:], 1.0, ["ones"])
+        for b in range(4):
+            op("g", lambda q, b=b: q.affine_select(T.eb[:, 512 * b:512 * b + 512], T.ones[:], [[-1, 512]], A.is_equal, 0.0, b, 4), ["ones"], [("eb", 512 * b, 512 * b + 512)])
+
+    def level(e, w_in, f, w_out, col, lst, lreads):
+        if e == "v":
+            vts(T[f][:], T[w_in][:], cc(col), None, A.add, None, [w_in, "ct"], [f])
+        else:
+            act(T[f][:], T[w_in][:], [w_in, "ct"], [f], bias=cc(col))
+
+    def merge(w_in, f, w_out, lst, lreads):
+        vtt(T[w_out][:], T[f][:].indirect(lst), T[w_in][:], A.min, [f, w_in] + lreads, [w_out])
+
+    state = ["x0", "xa1", "xa2", "xa3"]
+    for r in range(NR):
+        p = part[r]
+        xn, xm = state[r], state[r + 1]
+        for i, (a, b) in enumerate(SP):
+            vtr(T.ps3[:, a // 16:b // 16, :], T.pb[:, 512 * i:512 * i + b - a], [("pb", i, i + 1)], [("ps3", a, b)])
+        vcp(T["sc%d" % r][:], T.ps3[:, :, 0], ["ps3"], ["sc%d" % r])
+        send(p, "a_sc%d" % r, T["tc%d" % r][:], T["sc%d" % r][:], ["sc%d" % r])
+        ld, lds = T["ld%d" % r][:], ["ld%d" % r]
+        lp2, lp3, lps = T["lp%d" % r][:, 0:24], T["lp%d" % r][:, 24:48], ["lp%d" % r]
+        le, les = T["le%d" % r][:], ["le%d" % r]
+        lg2, lg3, lgs = T["lg%d" % r][:, 0:24], T["lg%d" % r][:, 24:48], ["lg%d" % r]
+        for i, (a, b) in enumerate(SP):
+            vtt(T.wo0[:, a:b], T.pb[:, 512 * i:512 * i + b - a], T.tw0[:, a:b], A.max, [("pb", i, i + 1), "tw0"], [("wo0", a, b)])
+        level("v", "wo0", "fo", None, 0, None, None)
+        merge("wo0", "fo", "wo1", ld, lds)
+        if r == 0:
+            op("v", lambda q: q.tensor_copy(T.einv[:].indirect(T.le0[:]), T.iota[:]), ["iota", "le0"], ["einv"])
+        send_powers(r)
+        if r == 0:
+            rest_of_constants()
+        for t in range(4):
+            act(T.hx[:, C * t:C * t + C], T[xn][:, t:4 * C:4], [xn], [("hx", C * t, C * t + C)], scale=0.5)
+        if r == 0:
+            act(T.lr[:], T.iota[:].indirect(T.ln[:]), ["iota", "ln"], ["lr"])
+            act(T.lr2[:], T.lr[:].indirect(T.lrho2[:]), ["lr", "lrho2"], ["lr2"])
+            dma("y", "d_n", T.lo[:], T.lr2[0:128:16, :], ["lr2"], ["lo"])
+        level("v", "wo1", "fo", None, 1, None, None)
+        merge("wo1", "fo", "wo0", lp2, lps)
+        level("v", "wo0", "fo", None, 2, None, None)
+        for i in range(6):
+            if i % 2:
+                act(T.kt[:, :, i], T["tc%d" % r][:], ["tc%d" % r], [("kt", 0, 384, i)])
+            else:
+                vcp(T.kt[:, :, i], T["tc%d" % r][:], ["tc%d" % r], [("kt", 0, 384, i)])
+        vtr(T.wt0[:], T.kt[:], ["kt"], ["wt0"])
+        level("s", "wt0", "ft", None, 3, None, None)
+        merge("wo0", "fo", "wo1", lp3, lps)
+        merge("wt0", "ft", "wt1", le, les)
+        level("s", "wt1", "ft", None, 4, None, None)
+        act(T.wo0[:], T.wo1[:], ["wo1", "ct"], ["wo0"], scale=cc(6), bias=cc(7))
+        merge("wt1", "ft", "wt0", lg2, lgs)
+        level("s", "wt0", "ft", None, 5, None, None)
+        vtr(T.po3[:], T.wo0[:], ["wo0"], ["po3"])
+        if r == 0:
+            vcp(T.lnr[:], T.lo[:], ["lo"], ["lnr"])
+            mates_list(0)
+        merge("wt0", "ft", "wt1", lg3, lgs)
+        act(T.base[:, 0:48:2], T.po3[:, :, 8], [("po3", 0, 384, "x")], [("base", 0, 48, 0)])
+        vts(T.vv[:], T.wt1[:].indirect(T.ln[:]), cc(6), cc(8), A.mult, A.add, ["wt1", "ln", "ct"], ["vv"])
+        ss = [("po3", 0, 384, "s")]
+        vtt(T.po3[:, :, 2:6:3], T.po3[:, :, 2:6:3], T.po3[:, :, 1:5:3], A.min, ss, ss)
+        vtt(T.po3[:, :, 4], T.po3[:, :, 4], T.po3[:, :, 2], A.min, ss, ss)
+        vtr(T.pt3[:], T.vv[:], ["vv"], ["pt3"])
+        act(T.base[:, 1:48:2], T.pt3[:, :, 8], [("pt3", 0, 384, "x")], [("base", 0, 48, 1)])
+        ss = [("pt3", 0, 384, "s")]
+        vtt(T.pt3[:, :, 0:4:3], T.pt3[:, :, 0:4:3], T.pt3[:, :, 1:5:3], A.min, ss, ss)
+        vtt(T.pt3[:, :, 1], T.pt3[:, :, 1], T.pt3[:, :, 3], A.min, ss, ss)
+        vtt(T.c6[:], T.po3[:, :, 0:6], T.pt3[:, :, 0:6], A.is_gt, [("po3", 0, 384, "s"), ("pt3", 0, 384, "s")], ["c6"])
+        vtt(T.m6[:, 0:48:2, :], T.c6[:], T.po3[:, :, 9:15], A.mult, ["c6", ("po3", 0, 384, "x")], [("m6", 0, 288, 0)])
+        vtt(T.m6[:, 1:48:2, :], T.c6[:], T.pt3[:, :, 9:15], A.mult, ["c6", ("pt3", 0, 384, "x")], [("m6", 0, 288, 1)])
+        vtt(T.m3[:], T.m6[:, :, 0:3], T.m6[:, :, 3:6], A.max, ["m6"], ["m3"])
+        vtt(T.m1[:], T.m3[:, :, 0], T.m3[:, :, 1], A.max, ["m3"], ["m1"])
+        vtt(T.m2[:], T.m3[:, :, 2], T.base[:], A.max, ["m3", "base"], ["m2"])
+        vtt(T.m0[:], T.m1[:], T.m2[:], A.max, ["m1", "m2"], ["m0"])
+        vts(T.tk[:], T.m0[:], 1.0 / 1024.0, MAGIC, A.mult, A.add, ["m0"], ["tk"])
+        vts(T.m1[:], T.tk[:], -MAGIC, -1024.0, A.add, A.mult, ["tk"], ["m1"])
+        vts(T.ab[:, :, 2], T.tk[:, 0:48:2], -MAGIC, None, A.add, None, ["tk"], [("ab", 0, 72, 1)])
+        vtt(T.ab[:, :, 0:2], T.m0[:], T.m1[:], A.add, ["m0", "m1"], [("ab", 0, 72, 0)])
+        vtt(T.kp[:, :, 0:3], T.ab[:], T.mo[:], A.mult, ["ab", "mo"], [("kp", 0, 384, 0)])
+        act(T.kp[:, :, 3], T.ab[:, :, 2], ["ab"], [("kp", 0, 384, 1)])
+        vtt(T.ai[:], T.ab[:], T.mi[:], A.mult, ["ab", "mi"], ["ai"])
+        vtr(T.rk[:, 16:400], T.kp[:], ["kp"], ["rk"])
+        vtr(T.qk[:], T.rk[:], ["rk"], ["qk"])
+        vtt(T.oab[:], T.ai[:], T.qk[:, 1:25, 0:3], A.add, ["ai", "qk"], ["oab"])
+        vts(T.la[:], T.oab[:, 0:72:3], 192.0, None, A.add, None, ["oab"], ["la"])
+        vts(T.lb[:], T.oab[:, 1:72:3], 192.0, None, A.add, None, ["oab"], ["lb"])
+        vcp(T.knr[:], T.rk[:, 16:400].indirect(T.lnr[:]), ["rk", "lnr"], ["knr"])
+        dma("y", "d_kn%d" % r, T.kno[:], T.knr[3:128:16, :], ["knr"], ["kno"])
+        for i, (a, b) in enumerate(ZP):
+            for t in range(4):
+                act(T.za[:, C * t + a:C * t + b], T.hx[:, C * t:C * t + C].indirect(T.la[:, a // 16:b // 16]),
+                    [("hx", C * t, C * t + C), "la"], [("za", C * t + a, C * t + b)])
+        hq, hqs = T["hq%d" % r], T["hqs%d" % r]
+        for i, (a, b) in enumerate(ZP):
+            for t in range(4):
+                vtt(T.zt[:, 4 * a + t:4 * b:4], T.hx[:, C * t:C * t + C].indirect(T.lb[:, a // 16:b // 16]), T.za[:, C * t + a:C * t + b], A.add,
+                    [("hx", C * t, C * t + C), "lb", ("za", C * t + a, C * t + b)], [("zt", 4 * a, 4 * b, t)])
+            quant(T.zq[:, a:b], T.zqs[:, a:b], T.zt[:, 4 * a:4 * b], [("zt", 4 * a, 4 * b)], [("zq", a, b), ("zqs", a, b)])
+            for k in range(4):
+                mm(4 * i + k, b - a, T.wq[:, 128 * k:128 * k + 128], T.wqs[:, 128 * k:128 * k + 128], T.zq[:, a:b], T.zqs[:, a:b],
+                   ["wq", "wqs", ("zq", a, b), ("zqs", a, b)])
+
+        def hcopy(e, i, k):
+            a, b = HP[i]
+            src = T.pb[:, 512 * (4 * i + k):512 * (4 * i + k) + b - a]
+            rd, wr = [("pb", 4 * i + k, 4 * i + k + 1)], [("ht", 4 * a, 4 * b, k)]
+            if e == "s":
+                act(T.ht[:, 4 * a + k:4 * b:4], src, rd, wr, scale=0.03125)
+            else:
+                vts(T.ht[:, 4 * a + k:4 * b:4], src, 0.03125, None, A.mult, None, rd, wr)
+
+        def hpiece(i):
+            a, b = HP[i]
+            quant(hq[:, a:b], hqs[:, a:b], T.ht[:, 4 * a:4 * b], [("ht", 4 * a, 4 * b)], [("hq%d" % r, a, b), ("hqs%d" % r, a, b)])
+            sem = "a_h%d_%d" % (r, i)
+            send(p, sem, T["hl%d" % r][:, a:b].bitcast(dt.uint8), hq[:, a:b].bitcast(dt.uint8), [("hq%d" % r, a, b)])
+            send(p, sem, T["hls%d" % r][:, a:b], hqs[:, a:b], [("hqs%d" % r, a, b)])
+
+        for k, e in enumerate("sssv"):
+            hcopy(e, 0, k)
+        hpiece(0)
+        vtt(T.dd[:], T.dno[:], T.fd[:], A.subtract, ["dno", "fd"], ["dd"])
+        vtt(T.kk[:], T.oab[:, 2:72:3], T.kno[:], A.add, ["oab", "kno"], ["kk"])
+        vts(T.kf[:], T.kk[:], 1, None, A.bitwise_and, None, ["kk"], ["kf"])
+        vtt(T.ff[:], T.kf[:], T.dd[:], A.mult, ["kf", "dd"], ["ff"])
+        vtt(T.fd[:], T.ff[:], T.fd[:], A.add, ["ff", "fd"], ["fd"])
+        nl_ = "ld%d" % (r + 1) if r + 1 < NR else "ldf"
+        vcp(T[nl_][:], T.fd[:], ["fd"], [nl_])
+        if r + 1 < NR:
+            send_d(r + 1)
+        for k, e in enumerate("vsvs"):
+            hcopy(e, 1, k)
+        hpiece(1)
+        if r == 0:
+            quant(T.eq[:], T.eqs[:], T.eb[:], ["eb"], ["eq", "eqs"])
+            quant(T.vq[:], T.vqs[:], T.v0[:], ["v0"], ["vq", "vqs"])
+        act(T.lr[:], T.einv[:].indirect(T[nl_][:]), ["einv", nl_], ["lr"])
+        act(T.lr2[:], T.lr[:].indirect(T.lrho[:, 0:24]), ["lr", ("lrho", 0, 24)], ["lr2"])
+        dma("y", "d_l%d" % r, T.lo[:], T.lr2[0:128:16, :], ["lr2"], ["lo"])
+        a, b = ZP[1]
+        for k in range(4):
+            act(T.jt[:, C * k + FAR:C * k + C], T.pb[:, 512 * (4 + k) + FAR - a:512 * (4 + k) + C - a], [("pb", 4 + k, 5 + k)],
+                [("jt", C * k + FAR, C * k + C)], scale=0.03125)
+        if r + 1 < NR:
+            power1(r + 1)
+            op("v", lambda q: q.tensor_copy(T.einv[:].indirect(T["le%d" % (r + 1)][:]), T.iota[:]), ["iota", "le%d" % (r + 1)], ["einv"])
+        else:
+            act(T.rt[:, 0:C], T.iota[:].indirect(T.ldf[:]), ["iota", "ldf"], [("rt", 0, C)])
+            dma("y", "out", T.dn[:], T.rt[0:128:16, 0:C], [("rt", 0, C)], [])
+        hl, hls = T["hl%d" % r], T["hls%d" % r]
+        for i, (a, b) in enumerate(HP):
+            for k in range(4):
+                mm(4 * i + k, b - a, T.eq[:, 128 * k:128 * k + 128], T.eqs[:, 128 * k:128 * k + 128], hl[:, a:b], hls[:, a:b],
+                   ["eq", "eqs", ("hl%d" % r, a, b), ("hls%d" % r, a, b)])
+        for k in range(4):
+            for i, (a, b) in enumerate(HP):
+                rd, wr = [("pb", 4 * i + k, 4 * i + k + 1)], [("jt", C * k + a, C * k + b)]
+                src = T.pb[:, 512 * (4 * i + k):512 * (4 * i + k) + b - a]
+                act(T.jt[:, C * k + a:C * k + b], src, rd, wr)
+        vcp(T.ll[:], T.lo[:], ["lo"], ["ll"])
+        for i, (a, b) in enumerate(SP):
+            for t in range(4):
+                vtt(T[xm][:, 4 * a + t:4 * b:4], T.jt[:, C * t:C * t + C].indirect(T.ll[:, a // 16:b // 16]), T[xn][:, 4 * a + t:4 * b:4], A.add,
+                    [("jt", C * t, C * t + C), "ll", (xn, 4 * a, 4 * b)], [(xm, 4 * a, 4 * b, t)])
+            if r + 1 < NR:
+                score(xm, i)
+            else:
+                quant(T.xq[:, a:b], T.xqs[:, a:b], T[xm][:, 4 * a:4 * b], [(xm, 4 * a, 4 * b)], [("xq", a, b), ("xqs", a, b)])
+        if r + 1 < NR:
+            powers2(r + 1)
+            mates_list(r + 1)
+    dma("y", "out", T.oc[:], T.xq[:].bitcast(dt.uint8), ["xq"], [])
+    for k in range(4):
+        dma("y", "out", T.osc[4 * k:4 * k + 4, :], T.xqs[32 * k:32 * k + 4, :], ["xqs"], [])
+    for i in range(2):
+        mm(i, 192, T.vq[:], T.vqs[:], T.xq[:, 192 * i:192 * i + 192], T.xqs[:, 192 * i:192 * i + 192], ["vq", "vqs", "xq", "xqs"])
+    act(T.ysb[:, 0:192], T.pb[:, 0:192], [("pb", 0, 1)], [("ysb", 0, 192)])
+    vcp(T.ysb[:, 192:384], T.pb[:, 512:704], [("pb", 1, 2)], [("ysb", 192, 384)])
+    dma("y", "out", T.y[:], T.ysb[:], ["ysb"], [])
+    for s, v in total.items():
+        need("g", (s, v))

@@ -1,120 +1,65 @@
+import numpy as np
 from concourse.mybir import AluOpType as A, ActivationFunctionType as F, dt
 
 C, FAR, NR = 384, 288, 3
 MASKS = [1, 2, 4]
-ZP = [(0, 160), (160, 384)]
 HP = [(0, 160), (160, 288)]
-SP = [(0, 192), (192, 384)]
+SP = [(0, 256), (256, 384)]
+HALF = [(0, 192), (192, 384)]
 HUGE = 1e29
 ONE = 2.0 ** 80
-MAGIC = 1.5 * 2.0 ** 23
-L1, L2, L3 = {1, 3, 4, 6}, {2, 3, 5, 6}, {4, 5, 6}
+BIG = 8192.0
+MID = 192.0
+s_ = np.s_
 
-SCRATCH = {
-    "x0": ("sbuf", [128, 4 * C], "bfloat16"),
-    "xa1": ("sbuf", [128, 4 * C], "bfloat16"),
-    "xa2": ("sbuf", [128, 4 * C], "bfloat16"),
-    "xa3": ("sbuf", [128, 4 * C], "bfloat16"),
-    "hx": ("sbuf", [128, 4 * C], "bfloat16"),
-    "za": ("sbuf", [128, 4 * C], "bfloat16"),
-    "zt": ("sbuf", [128, 4 * C], "bfloat16"),
-    "ht": ("sbuf", [128, 4 * FAR], "bfloat16"),
-    "jt": ("sbuf", [128, 4 * C], "bfloat16"),
-    "u0": ("sbuf", [128, 512], "bfloat16"),
-    "v0": ("sbuf", [128, 512], "bfloat16"),
-    "ones": ("sbuf", [128, 512], "bfloat16"),
-    "eb": ("sbuf", [128, 2048], "bfloat16"),
-    "kp": ("sbuf", [128, 24, 16], "bfloat16"),
-    "rk": ("sbuf", [128, 416], "bfloat16"),
-    "qk": ("sbuf", [128, 26, 16], "bfloat16"),
-    "pb": ("psum", [128, 4096], "float32"),
-    "dli": ("sbuf", [128, 24], "int32"),
-    "nli": ("sbuf", [128, 24], "int32"),
-    "ia": ("sbuf", [128, 24], "int32"),
-    "ib": ("sbuf", [128, 24], "int32"),
-    "ic": ("sbuf", [128, 24], "int32"),
-    "im": ("sbuf", [128, 72], "int32"),
-    "iu": ("sbuf", [128, 8], "int32"),
-    "ij": ("sbuf", [128, 24], "int32"),
-    "ik": ("sbuf", [128, 24], "int32"),
-    "kk": ("sbuf", [128, 24], "int32"),
-    "kf": ("sbuf", [128, 24], "int32"),
-    "lu": ("sbuf", [128, 8], "uint16"),
-    "lrho": ("sbuf", [128, 48], "uint16"),
-    "lrho2": ("sbuf", [128, 24], "uint16"),
-    "ln": ("sbuf", [128, 24], "uint16"),
-    "lnr": ("sbuf", [128, 24], "uint16"),
-    "la": ("sbuf", [128, 24], "uint16"),
-    "lb": ("sbuf", [128, 24], "uint16"),
-    "ll": ("sbuf", [128, 24], "uint16"),
-    "vt": ("sbuf", [128, 22, 16], "float32"),
-    "ct": ("sbuf", [128, 352], "float32"),
-    "kt": ("sbuf", [128, 24, 16], "float32"),
-    "ps3": ("sbuf", [128, 24, 16], "float32"),
-    "po3": ("sbuf", [128, 24, 16], "float32"),
-    "pt3": ("sbuf", [128, 24, 16], "float32"),
-    "c6": ("sbuf", [128, 24, 6], "float32"),
-    "m6": ("sbuf", [128, 48, 6], "float32"),
-    "m3": ("sbuf", [128, 48, 3], "float32"),
-    "m1": ("sbuf", [128, 48], "float32"),
-    "m2": ("sbuf", [128, 48], "float32"),
-    "m0": ("sbuf", [128, 48], "float32"),
-    "tk": ("sbuf", [128, 48], "float32"),
-    "ab": ("sbuf", [128, 24, 3], "float32"),
-    "ai": ("sbuf", [128, 72], "float32"),
-    "oab": ("sbuf", [128, 72], "float32"),
-    "base": ("sbuf", [128, 48], "float32"),
-    "mo": ("sbuf", [128, 72], "float32"),
-    "mi": ("sbuf", [128, 72], "float32"),
-    "iota": ("sbuf", [128, C], "float32"),
-    "tw0": ("sbuf", [128, C], "float32"),
-    "wo0": ("sbuf", [128, C], "float32"),
-    "wo1": ("sbuf", [128, C], "float32"),
-    "fo": ("sbuf", [128, C], "float32"),
-    "wt0": ("sbuf", [128, C], "float32"),
-    "wt1": ("sbuf", [128, C], "float32"),
-    "ft": ("sbuf", [128, C], "float32"),
-    "vv": ("sbuf", [128, C], "float32"),
-    "einv": ("sbuf", [128, C], "float32"),
-    "knr": ("sbuf", [128, C], "float32"),
-    "kno": ("sbuf", [128, 24], "float32"),
-    "lr": ("sbuf", [128, C], "float32"),
-    "lr2": ("sbuf", [128, C], "float32"),
-    "lo": ("sbuf", [128, 24], "float32"),
-    "rt": ("sbuf", [128, 3 * C], "float32"),
-    "rq": ("sbuf", [128, 2 * C], "float32"),
-    "rqd": ("sbuf", [128, C], "float32"),
-    "od23": ("sbuf", [128, 48], "float32"),
-    "dno": ("sbuf", [128, 24], "float32"),
-    "dd": ("sbuf", [128, 24], "float32"),
-    "fd": ("sbuf", [128, 24], "float32"),
-    "ff": ("sbuf", [128, 24], "float32"),
-    "fg": ("sbuf", [128, 24], "float32"),
-    "ysb": ("sbuf", [128, C], "float32"),
-    "uq": ("sbuf", [128, 128], "float8_e4m3fn_x4"), "uqs": ("sbuf", [128, 128], "uint8"),
-    "ur": ("sbuf", [128, 128], "float8_e4m3fn_x4"), "urs": ("sbuf", [128, 128], "uint8"),
-    "vq": ("sbuf", [128, 128], "float8_e4m3fn_x4"), "vqs": ("sbuf", [128, 128], "uint8"),
-    "wq": ("sbuf", [128, 512], "float8_e4m3fn_x4"), "wqs": ("sbuf", [128, 512], "uint8"),
-    "eq": ("sbuf", [128, 512], "float8_e4m3fn_x4"), "eqs": ("sbuf", [128, 512], "uint8"),
-    "xq": ("sbuf", [128, C], "float8_e4m3fn_x4"), "xqs": ("sbuf", [128, C], "uint8"),
-    "zq": ("sbuf", [128, C], "float8_e4m3fn_x4"), "zqs": ("sbuf", [128, C], "uint8"),
-}
-SEMAPHORES = ["cv", "cs", "ct", "cg", "loc", "out"]
-LOADS = ["x", "u", "v", "wc", "wsp", "dl", "nl"]
-SEMAPHORES += ["ld_" + k for k in LOADS] + ["d_n"]
+SCRATCH = {}
+
+
+def declare(dtype, shape, names, where="sbuf"):
+    for name in names.split():
+        SCRATCH[name] = (where, [128] + shape, dtype)
+
+
+declare("bfloat16", [4 * C], "x0 xa1 xa2 xa3 hx za zt jt")
+declare("bfloat16", [4 * FAR], "ht")
+declare("bfloat16", [512], "u0 v0")
+declare("bfloat16", [516], "ones dg")
+declare("bfloat16", [24, 16], "kp kn ti tl")
+declare("bfloat16", [C], "rk rn ri rl")
+declare("float32", [4096], "pb", "psum")
+declare("int32", [24], "dli nli ki kj")
+declare("int32", [8], "iu")
+declare("int32", [48], "ni nj")
+declare("uint16", [8], "lu")
+declare("uint16", [24], "ln la lb ll l3 m3 li ldf")
+declare("float32", [24, 16], "ko k1 kt po2 po3 pt")
+declare("float32", [2, 2, 16], "vt")
+declare("float32", [64], "ct")
+declare("float32", [24], "cT")
+declare("float32", [C], "iota tw0 tw1 v0t v1t v2t w1 w2 w3 fo wt ft wu vv r1 ysb")
+declare("float32", [168], "c8 da db")
+declare("float32", [24, 3], "odd dlt prd")
+declare("float32", [448], "sa")
+declare("float32", [16, 2, 3], "new")
+declare("float32", [64, 2], "fl ol")
+declare("float32", [4, 2, 16], "r5")
+declare("float32", [2, 2, 16], "r4a r4b r4c")
+declare("float32", [32, 2], "oa")
+declare("float32", [16, 2, 2], "ob oe")
+for _n, _w in (("uq", 128), ("ur", 128), ("vq", 128), ("wq", 512), ("eq", 512), ("xq", C), ("zq", FAR), ("zo", 128)):
+    declare("float8_e4m3fn_x4", [_w], _n)
+    declare("uint8", [_w], _n + "s")
+SEMAPHORES = ["cv", "cs", "ct", "cg", "loc", "out"] + ["ld_" + k for k in ("x0", "x1", "u", "v", "wc", "wsp", "dl", "nl")]
 for _r in range(NR):
-    SCRATCH["sc%d" % _r] = ("sbuf", [128, 24], "float32")
-    SCRATCH["tc%d" % _r] = ("sbuf", [128, 24], "float32")
-    SCRATCH["ld%d" % _r] = ("sbuf", [128, 24], "uint16")
-    SCRATCH["lp%d" % _r] = ("sbuf", [128, 48], "uint16")
-    SCRATCH["le%d" % _r] = ("sbuf", [128, 24], "uint16")
-    SCRATCH["lg%d" % _r] = ("sbuf", [128, 48], "uint16")
+    declare("float32", [24, 5], "sc%d" % _r)
+    declare("float32", [16, 2, 5], "tc%d" % _r)
+    declare("uint16", [24], "ld%d le%d" % (_r, _r))
+    declare("bfloat16", [24], "ls%d lm%d" % (_r, _r))
     for _k in ("hq", "hl"):
-        SCRATCH["%s%d" % (_k, _r)] = ("sbuf", [128, FAR], "float8_e4m3fn_x4")
-        SCRATCH["%ss%d" % (_k, _r)] = ("sbuf", [128, FAR], "uint8")
-    SEMAPHORES += [k + str(_r) for k in ("a_sc", "a_le", "a_lg", "d_p2_", "d_p3_", "d_dn", "d_kn", "d_l")]
+        declare("float8_e4m3fn_x4", [FAR], "%s%d" % (_k, _r))
+        declare("uint8", [FAR], "%ss%d" % (_k, _r))
+    SEMAPHORES += [k + str(_r) for k in ("a_sc", "a_le", "a_lm")]
     SEMAPHORES += ["a_h%d_%d" % (_r, p) for p in range(len(HP))]
-SCRATCH["ldf"] = ("sbuf", [128, 24], "uint16")
 
 
 def rank_program(g, core, T, topo):
@@ -124,6 +69,28 @@ def rank_program(g, core, T, topo):
     que = {"v": g.vector, "s": g.scalar, "t": g.tensor, "g": g, "y": g.sync}
     total, know, recs = {}, {}, {}
     clk = {e: {} for e in que}
+
+    def a(name, idx=None):
+        shape = SCRATCH[name][1]
+        idx = s_[:] if idx is None else idx
+        at = np.arange(int(np.prod(shape[1:]))).reshape([1] + shape[1:])[(slice(None),) + (idx[1:] if isinstance(idx, tuple) else ())]
+        m = np.zeros(int(np.prod(shape[1:])), bool)
+        m[at.reshape(-1)] = True
+        if name == "pb":
+            m = np.repeat(m.reshape(8, 512).any(axis=1), 512)
+        return (T[name][idx], [(name, m)])
+
+    def cols(name, lo, hi):
+        return a(name, s_[:, lo:hi])
+
+    def by(win, off):
+        return (win[0].indirect(off[0]), win[1] + off[1])
+
+    def raw(x, kind):
+        return (x[0].bitcast(kind), x[1])
+
+    def hbm(ap):
+        return (ap, [])
 
     def need(e, ev):
         sem, val = ev
@@ -136,423 +103,404 @@ def rank_program(g, core, T, topo):
             if c.get(k, 0) < w:
                 c[k] = w
 
-    def reg(r):
-        r = (r,) if isinstance(r, str) else r
-        return (r[0], r[1] if len(r) > 1 else 0, r[2] if len(r) > 2 else 1 << 30, r[3] if len(r) > 3 else None)
-
     def hazards(e, rd, wr):
-        evs = []
-        for w, regs in ((False, rd), (True, wr)):
-            for r in regs:
-                n, lo, hi, ph = reg(r)
-                for (l2, h2, p2, w2, ev, e2) in recs.get(n, ()):
-                    if l2 < hi and lo < h2 and (ph is None or p2 is None or ph == p2) and (w or w2 or (n == "pb" and e2 != e)):
-                        evs.append(ev)
         best = {}
-        for s, v in evs:
-            best[s] = max(best.get(s, 0), v)
+        for w, regs in ((False, rd), (True, wr)):
+            for n, m in regs:
+                for (m2, w2, ev, e2) in recs.get(n, ()):
+                    if (w or w2 or (n == "pb" and e2 != e)) and (m & m2).any():
+                        best[ev[0]] = max(best.get(ev[0], 0), ev[1])
         for s in sorted(best, key=lambda k: -best[k]):
             need(e, (s, best[s]))
 
     def note(e, rd, wr, ev):
-        for r in wr:
-            n, lo, hi, ph = reg(r)
-            recs[n] = [x for x in recs.get(n, []) if not (lo <= x[0] and x[1] <= hi and (ph is None or x[2] == ph))]
-            recs[n].append((lo, hi, ph, True, ev, e))
-        for r in rd:
-            n, lo, hi, ph = reg(r)
-            recs[n] = [x for x in recs.get(n, []) if x[3] or x[5] != e or x[:3] != (lo, hi, ph) or x[4][0] != ev[0]]
-            recs[n].append((lo, hi, ph, False, ev, e))
+        for n, m in wr:
+            recs[n] = [x for x in recs.get(n, []) if (x[0] & ~m).any()] + [(m, True, ev, e)]
+        for n, m in rd:
+            recs[n] = [x for x in recs.get(n, []) if x[1] or x[2][0] != ev[0] or (x[0] & ~m).any()] + [(m, False, ev, e)]
 
-    def op(e, fn, rd, wr):
+    def issue(e, sem, step, fn, ins, outs):
+        rd = [r for x in ins if isinstance(x, tuple) for r in x[1]]
+        wr = [r for x in outs for r in x[1][:1]]
+        rd += [r for x in outs for r in x[1][1:]]
         hazards(e, rd, wr)
-        sem = "c" + e
-        total[sem] = total.get(sem, 0) + 1
+        total[sem] = total.get(sem, 0) + step
         ev = (sem, total[sem])
         know[ev] = dict(clk[e])
-        fn(que[e]).then_inc(T.sem[sem], 1)
+        fn(que[e]).then_inc(T.sem[sem], step)
         note(e, rd, wr, ev)
 
-    def dma(e, sem, out, in_, rd, wr):
-        hazards(e, rd, wr)
-        total[sem] = total.get(sem, 0) + 16
-        ev = (sem, total[sem])
-        know[ev] = dict(clk[e])
-        que[e].dma_start(out, in_).then_inc(T.sem[sem], 16)
-        note(e, rd, wr, ev)
+    def op(e, fn, ins, outs):
+        if e == "g" and "cg" in total:
+            need("g", ("cg", total["cg"]))
+        issue(e, "c" + e, 1, fn, ins, outs)
 
-    def send(dst, sem, out, in_, rd):
-        hazards("g", rd, [])
+    def dma(e, sem, out, in_):
+        issue(e, sem, 16, lambda q: q.dma_start(out[0], in_[0]), [in_], [out])
+
+    def send(dst, sem, out, in_):
+        hazards("g", in_[1], [])
         rid, pid, _ = topo.addr(dst)
-        g.remote_dma(out, in_, T.sem[sem], T.sem["loc"], pid, rid, topo.mask(core, dst))
+        g.remote_dma(out[0], in_[0], T.sem[sem], T.sem["loc"], pid, rid, topo.mask(core, dst))
         total["loc"] = total.get("loc", 0) + len(topo.engines(core, dst))
 
-    def lands(src, sem, times, names):
-        total[sem] = times * len(topo.engines(src, core))
-        for n in names:
-            recs.setdefault(n, []).append((n_lo(n), n_hi(n), None, True, (sem, total[sem]), "remote") if isinstance(n, str) else None)
-
-    def n_lo(n):
-        return 0
-
-    def n_hi(n):
-        return 1 << 30
-
-    def land_cols(src, sem, times, regs):
-        total[sem] = times * len(topo.engines(src, core))
-        for r in regs:
-            n, lo, hi, ph = reg(r)
-            recs.setdefault(n, []).append((lo, hi, None, True, (sem, total[sem]), "remote"))
+    def lands(src, sem, what):
+        total[sem] = len(what) * len(topo.engines(src, core))
+        for x in what:
+            for n, m in x[1]:
+                recs.setdefault(n, []).append((m, True, (sem, total[sem]), "remote"))
 
     part = [T.cores[rank ^ m] for m in MASKS]
     for r in range(NR):
-        p = part[r]
-        land_cols(p, "a_sc%d" % r, 1, ["tc%d" % r])
-        land_cols(p, "a_le%d" % r, 1, ["le%d" % r])
-        land_cols(p, "a_lg%d" % r, 1, ["lg%d" % r])
-        for i, (a, b) in enumerate(HP):
-            land_cols(p, "a_h%d_%d" % (r, i), 2, [("hl%d" % r, a, b), ("hls%d" % r, a, b)])
+        lands(part[r], "a_sc%d" % r, [a("tc%d" % r, s_[:, 0:12])])
+        lands(part[r], "a_le%d" % r, [a("le%d" % r)])
+        lands(part[r], "a_lm%d" % r, [a("lm%d" % r)])
+        for i, (lo, hi) in enumerate(HP):
+            lands(part[r], "a_h%d_%d" % (r, i), [cols("hl%d" % r, lo, hi), cols("hls%d" % r, lo, hi)])
 
-    def vts(out, in0, s1, s2, o0, o1, rd, wr):
+    def val(x):
+        return x[0] if isinstance(x, tuple) else x
+
+    def ts(out, in0, s1, o0, s2=None, o1=None):
         if o1 is None:
-            op("v", lambda q: q.tensor_scalar(out, in0, s1, None, o0), rd, wr)
+            op("v", lambda q: q.tensor_scalar(out[0], in0[0], val(s1), None, o0), [in0, s1], [out])
         else:
-            op("v", lambda q: q.tensor_scalar(out, in0, s1, s2, o0, o1), rd, wr)
+            op("v", lambda q: q.tensor_scalar(out[0], in0[0], val(s1), val(s2), o0, o1), [in0, s1, s2], [out])
 
-    def vtt(out, a, b, o, rd, wr):
-        op("v", lambda q: q.tensor_tensor(out, a, b, o), rd, wr)
+    def tt(out, x, y, o):
+        op("v", lambda q: q.tensor_tensor(out[0], x[0], y[0], o), [x, y], [out])
 
-    def vcp(out, in_, rd, wr):
-        op("v", lambda q: q.tensor_copy(out, in_), rd, wr)
+    def cp(out, in_):
+        op("v", lambda q: q.tensor_copy(out[0], in_[0]), [in_], [out])
 
-    def vms(ap, c, wr):
-        op("v", lambda q: q.memset(ap, c), [], wr)
+    def fill(out, c):
+        op("v", lambda q: q.memset(out[0], c), [], [out])
 
-    def vtr(out, in_, rd, wr):
-        op("v", lambda q: q.transpose(out, in_), rd, wr)
+    def turn(out, in_):
+        op("v", lambda q: q.transpose(out[0], in_[0]), [in_], [out])
 
-    def act(out, in_, rd, wr, scale=None, bias=None):
+    def scan(out, d0, d1):
+        op("v", lambda q: q.tensor_tensor_scan(out[0], d0[0], d1[0], 0.0, A.mult, A.max), [d0, d1], [out])
+
+    def act(out, in_, scale=None, bias=None):
         if bias is not None:
-            op("s", lambda q: q.activation(out, in_, F.Identity, bias=bias, scale=1.0 if scale is None else scale), rd, wr)
+            op("s", lambda q: q.activation(out[0], in_[0], F.Identity, bias=val(bias), scale=1.0 if scale is None else scale), [in_, bias], [out])
         elif scale is not None:
-            op("s", lambda q: q.activation(out, in_, F.Copy, scale=scale), rd, wr)
+            op("s", lambda q: q.activation(out[0], in_[0], F.Copy, scale=scale), [in_], [out])
         else:
-            op("s", lambda q: q.activation(out, in_, F.Copy), rd, wr)
+            op("s", lambda q: q.activation(out[0], in_[0], F.Copy), [in_], [out])
 
-    def quant(q_, s_, in_, rd, wr):
-        op("v", lambda q: q.quantize_mx(q_, s_, in_), rd, wr)
+    def move(e, out, in_, scale=None):
+        if e == "s":
+            act(out, in_, scale)
+        elif scale is None:
+            cp(out, in_)
+        else:
+            ts(out, in_, scale, A.mult)
 
-    def mm(bank, w, l, ls, r_, rs, rd):
-        op("t", lambda q: q.matmul_mx(T.pb[:, 512 * bank:512 * bank + w], l, ls, r_, rs, True, True), rd, [("pb", bank, bank + 1)])
+    def quant(name, lo, hi, in_):
+        q_, p_ = cols(name[0], lo, hi), cols(name[1], lo, hi)
+        op("v", lambda q: q.quantize_mx(q_[0], p_[0], in_[0]), [in_], [q_, p_])
 
-    def cc(k):
-        return T.ct[:, 32 * k:32 * k + 1]
+    def bank(k, lo, hi):
+        return cols("pb", 512 * k + lo, 512 * k + hi)
 
-    dma("y", "ld_dl", T.dli[:], T.dl[:], [], ["dli"])
-    dma("s", "ld_u", T.u0[:], T.u[:], [], ["u0"])
-    dma("y", "ld_x", T.x0[:], T.x[:], [], ["x0"])
-    dma("s", "ld_nl", T.nli[:], T.nl[:], [], ["nli"])
-    dma("y", "ld_wc", T.wq[:].bitcast(dt.uint8), T.wc[:], [], ["wq"])
-    dma("y", "ld_wsp", T.wqs[:], T.ws[:], [], ["wqs"])
-    dma("y", "ld_v", T.v0[:], T.v[:], [], ["v0"])
+    def mm(k, left, l0, right, lo, hi):
+        x = [cols(left[0], l0, l0 + 128), cols(left[1], l0, l0 + 128), cols(right[0], lo, hi), cols(right[1], lo, hi)]
+        out = bank(k, 0, hi - lo)
+        op("t", lambda q: q.matmul_mx(out[0], x[0][0], x[1][0], x[2][0], x[3][0], True, True), x, [out])
 
-    def iota(name, pattern, cm, fl=False):
+    def iota(out, pattern, base, cm, fl=False):
         if fl:
-            op("g", lambda q: q.iota(T[name][:], pattern, 0, cm, allow_small_or_imprecise_dtypes=True), [], [name])
+            op("g", lambda q: q.iota(out[0], pattern, base, cm, allow_small_or_imprecise_dtypes=True), [], [out])
         else:
-            op("g", lambda q: q.iota(T[name][:], pattern, 0, cm), [], [name])
+            op("g", lambda q: q.iota(out[0], pattern, base, cm), [], [out])
 
-    iota("iota", [[1, C]], 0, True)
-    iota("iu", [[16, 8]], 0)
-    iota("ia", [[16, 24]], 0)
-    iota("ib", [[0, 24]], 1)
-    iota("ic", [[32, 12], [0, 2]], 0)
-    iota("im", [[16, 24], [0, 3]], 1)
+    def row(name, lo, hi=None, step=1):
+        return a(name, s_[:, :, lo] if hi is None else s_[:, :, lo:hi:step])
 
-    own_q = [q if q < 6 else None for q in range(8)] + [q if q < 7 else None for q in range(8)]
-    far_q = [5 - q if q < 6 else None for q in range(8)] + [6 - q if q < 7 else None for q in range(8)]
+    def blocks(name, lo, hi):
+        return a(name, s_[:, lo // 16:hi // 16, :])
 
-    def bias(qs, lv):
-        return [HUGE if q is None or q not in lv else (0.0 if r < 8 else -1024.0 * ONE) for r, q in enumerate(qs)]
+    def offs(name, lo, hi):
+        return cols(name, lo // 16, hi // 16)
 
-    def dec(qs):
-        return [0.0 if r < 8 else (1024.0 * sum(q in lv for lv in (L1, L2, L3)) if q is not None else 0.0) - 4096.0 + 1024.0 * (r - 7) - 192.0 for r, q in enumerate(qs)]
+    def swap1(mid, src):
+        for h in range(2):
+            turn(a(mid, s_[:, :, h, :]), src(h))
 
-    cols = [bias(own_q, L1), bias(own_q, L2), bias(own_q, L3), bias(far_q, L1), bias(far_q, L2), bias(far_q, L3),
-            [1.0] * 8 + [1.0 / ONE] * 8, dec(own_q), dec(far_q), [0.0] * 8 + [ONE] * 8, [-HUGE] * 8 + [4096.0 * ONE] * 8]
+    def swap2(dst, mid):
+        for m in range(2):
+            turn(dst(m), a(mid, s_[:, m::2, :, :]))
 
-    def d_lists(r):
-        return T["ld%d" % r][:] if r < NR else T.ldf[:]
+    UQ, UR, VQ, WQ, EQ, XQ, ZQ, ZO = [(n, n + "s") for n in ("uq", "ur", "vq", "wq", "eq", "xq", "zq", "zo")]
+    fbias, vbias = cols("ct", 0, 1), cols("ct", 32, 33)
 
-    def first_list():
-        vcp(T["ld0"][:], T.dli[:], ["dli"], ["ld0"])
+    dma("y", "ld_dl", a("dli"), hbm(T.dl[:]))
+    dma("s", "ld_u", a("u0"), hbm(T.u[:]))
+    for i, (lo, hi) in enumerate(SP):
+        dma("ys"[i], "ld_x%d" % i, cols("x0", 4 * lo, 4 * hi), hbm(T.x[:, 4 * lo:4 * hi]))
+    dma("s", "ld_nl", a("nli"), hbm(T.nl[:]))
+    dma("y", "ld_wc", raw(a("wq"), dt.uint8), hbm(T.wc[:]))
+    dma("y", "ld_wsp", a("wqs"), hbm(T.ws[:]))
+    dma("y", "ld_v", a("v0"), hbm(T.v[:]))
 
-    vms(T.vt[:], HUGE, ["vt"])
-    for k, vals in enumerate(cols):
-        r0 = 0
-        if k == 4:
-            first_list()
-        while r0 < 16:
-            r1 = r0
-            while r1 < 16 and vals[r1] == vals[r0]:
-                r1 += 1
-            if vals[r0] != HUGE:
-                a0, a1, val = r0, r1, float(vals[r0])
-                vms(T.vt[:, 2 * k:2 * k + 2, a0:a1], val, [("vt", 32 * k, 32 * k + 32, (k, r0))])
-            r0 = r1
-    vtr(T.ct[:], T.vt[:], ["vt"], ["ct"])
-    vts(T.tw0[:], T.iota[:], cc(9), cc(10), A.mult, A.add, ["iota", "ct"], ["tw0"])
-    vcp(T.fd[:], T.dli[:], ["dli"], ["fd"])
-    vcp(T.lu[:], T.iu[:], ["iu"], ["lu"])
-    vcp(T.ln[:], T.nli[:], ["nli"], ["ln"])
-    vts(T.ij[:], T.ib[:], 15, None, A.bitwise_and, None, ["ib"], ["ij"])
-    vtt(T.ij[:], T.ij[:], T.ia[:], A.add, ["ij", "ia"], ["ij"])
+    fill(a("ones"), 1.0)
+    for k in range(4):
+        iota(a("cT", s_[32 * k:32 * k + 32, :]), [[32, 12], [0, 2]], 0, 1, True)
+    iota(a("iu"), [[16, 8]], 0, 0)
+    iota(a("iota"), [[1, C]], -int(MID), 0, True)
+    op("g", lambda q: q.affine_select(T.dg[:], T.ones[:], [[-1, 516]], A.is_equal, 0.0, 3, 4), [a("ones")], [a("dg")])
+    for name in ("vt", "ko", "k1"):
+        fill(a(name), HUGE)
+    fill(a("vt", s_[:, 0, :, 4:7]), 0.0)
+    fill(a("vt", s_[:, 0, :, 12:15]), -BIG * ONE)
+    fill(a("vt", s_[:, 1, :, 1:8]), 0.0)
+    for name, lo, hi in (("k1", 2, 4), ("k1", 5, 8), ("ko", 3, 4), ("ko", 6, 8)):
+        fill(row(name, lo, hi), -HUGE)
+    for name, r_, k in (("k1", 9, 1024.0), ("k1", 12, 4096.0 + BIG), ("ko", 10, 2048.0), ("ko", 13, 5120.0 + BIG), ("kt", 8, 0.0)):
+        ts(row(name, r_), a("cT"), k, A.add, ONE, A.mult)
+    turn(a("ct"), a("vt"))
+    cp(a("lu"), a("iu"))
+    turn(a("tw1"), a("k1"))
+    fill(a("kp"), 0.0)
 
-    def rho(dst_f):
-        vts(T.ff[:], T.ij[:], 1.0 / 24.0, -11.5 / 24.0, A.mult, A.add, ["ij"], ["ff"])
-        vcp(T.ik[:], T.ff[:], ["ff"], ["ik"])
-        vts(T.ff[:], T.ik[:], -383.0, None, A.mult, None, ["ik"], ["ff"])
-        vts(T.fg[:], T.ij[:], 16.0, None, A.mult, None, ["ij"], ["fg"])
-        vtt(T.ij[:], T.ff[:], T.fg[:], A.add, ["ff", "fg"], ["ij"])
+    def small_constants():
+        fill(row("kt", 0, 16, 15), HUGE)
+        fill(cols("sa", 336, 448), 0.0)
+        fill(a("new", s_[:, 12:16]), 0.0)
+        fill(a("fl", s_[:, 36:64, :]), 0.0)
+        ts(row("kp", 3), a("cT"), -MID, A.add)
 
-    rho(None)
-    vcp(T.lrho[:, 0:24], T.ij[:], ["ij"], [("lrho", 0, 24)])
-    vts(T.lrho[:, 24:48], T.ij[:], 384.0, None, A.add, None, ["ij"], [("lrho", 24, 48)])
-    rho(None)
-    vcp(T.lrho2[:], T.ij[:], ["ij"], ["lrho2"])
+    for r in range(NR):
+        fill(a("tc%d" % r, s_[:, 12:16]), 0.0)
 
-    def power1(r):
-        ld = T["ld%d" % r][:]
-        act(T.rt[:, 0:C], T.iota[:].indirect(ld), ["iota", "ld%d" % r], [("rt", 0, C)])
+    def newv(k):
+        return a("new", s_[:, 0:12, :, k])
 
-    def powers2(r):
-        ld = T["ld%d" % r][:]
-        act(T.rt[:, C:2 * C], T.rt[:, 0:C].indirect(ld), [("rt", 0, C), "ld%d" % r], [("rt", C, 2 * C)])
-        act(T.rt[:, 2 * C:3 * C], T.rt[:, C:2 * C].indirect(ld), [("rt", C, 2 * C), "ld%d" % r], [("rt", 2 * C, 3 * C)])
-        act(T.rq[:], T.rt[:, C:3 * C].indirect(T.lrho[:]), [("rt", C, 3 * C), "lrho"], ["rq"])
-        dma("y", "d_p2_%d" % r, T.od23[:, 0:24], T.rq[0:128:16, 0:C], ["rq"], [("od23", 0, 24)])
-        dma("y", "d_p3_%d" % r, T.od23[:, 24:48], T.rq[0:128:16, C:2 * C], ["rq"], [("od23", 24, 48)])
-
-    def mates_list(r):
-        act(T.rqd[:], T.rt[:, 0:C].indirect(T.lnr[:]), [("rt", 0, C), "lnr"], ["rqd"])
-        dma("y", "d_dn%d" % r, T.dno[:], T.rqd[0:128:16, :], ["rqd"], ["dno"])
+    def own_tables():
+        act(row("ko", 11), newv(0), ONE, (MID + 3072.0) * ONE)
+        act(row("ko", 14), newv(0), ONE, (MID + 6144.0 + BIG) * ONE)
 
     def send_d(r):
-        send(part[r], "a_le%d" % r, T["le%d" % r][:], T["ld%d" % r][:], ["ld%d" % r])
+        send(part[r], "a_le%d" % r, a("le%d" % r), a("ld%d" % r))
 
-    def send_powers(r):
-        vcp(T["lp%d" % r][:], T.od23[:], ["od23"], ["lp%d" % r])
-        send(part[r], "a_lg%d" % r, T["lg%d" % r][:], T["lp%d" % r][:], ["lp%d" % r])
+    def places_for_partner(r):
+        act(a("rl"), by(a("ri"), a("le%d" % r)))
 
-    send_d(0)
-    power1(0)
-    powers2(0)
-
-    quant(T.uq[:], T.uqs[:], T.u0[:], ["u0"], ["uq", "uqs"])
-    vcp(T.ur[:].bitcast(dt.uint32), T.uq[:].bitcast(dt.uint32).indirect(T.lu[:]), ["uq", "lu"], ["ur"])
-    vcp(T.urs[:], T.uqs[:].indirect(T.lu[:]), ["uqs", "lu"], ["urs"])
+    def unit(b):
+        quant(EQ, 128 * b, 128 * b + 128, cols("dg", 3 - b, 515 - b))
 
     def score(xn, i):
-        a, b = SP[i]
-        quant(T.xq[:, a:b], T.xqs[:, a:b], T[xn][:, 4 * a:4 * b], [(xn, 4 * a, 4 * b)], [("xq", a, b), ("xqs", a, b)])
-        mm(i, b - a, T.ur[:], T.urs[:], T.xq[:, a:b], T.xqs[:, a:b], ["ur", "urs", ("xq", a, b), ("xqs", a, b)])
+        lo, hi = SP[i]
+        quant(XQ, lo, hi, cols(xn, 4 * lo, 4 * hi))
+        mm(i, UR, 0, XQ, lo, hi)
 
+    cp(a("ld0"), a("dli"))
+    send_d(0)
+    act(a("r1"), by(a("iota"), a("ld0")))
+    quant(UQ, 0, 128, a("u0"))
+    cp(raw(a("ur"), dt.uint32), by(raw(a("uq"), dt.uint32), a("lu")))
+    act(a("urs"), by(a("uqs"), a("lu")))
+    small_constants()
+    turn(a("po3"), a("r1"))
+    cp(newv(0), row("po3", 0))
+    own_tables()
+    act(row("kp", 1), newv(0))
+    cp(by(a("ri"), a("ld0")), a("iota"))
     score("x0", 0)
+    turn(a("tw0"), a("ko"))
     score("x0", 1)
-
-    def rest_of_constants():
-        vts(T.ij[:], T.ib[:], 31, None, A.bitwise_and, None, ["ib"], ["ij"])
-        vtt(T.ff[:], T.ij[:], T.ic[:], A.add, ["ij", "ic"], ["ff"])
-        for i in range(8, 16):
-            vts(T.kt[:, :, i], T.ff[:], 4096.0, ONE, A.add, A.mult, ["ff"], [("kt", 0, 384, i)])
-        vms(T.kt[:, :, 6:8], 0.0, [("kt", 0, 384, 6)])
-        vts(T.im[:], T.im[:], 4, 1, A.logical_shift_right, A.bitwise_and, ["im"], ["im"])
-        vcp(T.mo[:], T.im[:], ["im"], ["mo"])
-        vts(T.mi[:], T.mo[:], -1.0, 1.0, A.mult, A.add, ["mo"], ["mi"])
-        vms(T.kp[:], 0.0, ["kp"])
-        vms(T.rk[:], 0.0, ["rk"])
-        vms(T.ones[:], 1.0, ["ones"])
-        for b in range(4):
-            op("g", lambda q, b=b: q.affine_select(T.eb[:, 512 * b:512 * b + 512], T.ones[:], [[-1, 512]], A.is_equal, 0.0, b, 4), ["ones"], [("eb", 512 * b, 512 * b + 512)])
-
-    def level(e, w_in, f, w_out, col, lst, lreads):
-        if e == "v":
-            vts(T[f][:], T[w_in][:], cc(col), None, A.add, None, [w_in, "ct"], [f])
-        else:
-            act(T[f][:], T[w_in][:], [w_in, "ct"], [f], bias=cc(col))
-
-    def merge(w_in, f, w_out, lst, lreads):
-        vtt(T[w_out][:], T[f][:].indirect(lst), T[w_in][:], A.min, [f, w_in] + lreads, [w_out])
+    cp(a("ln"), a("nli"))
 
     state = ["x0", "xa1", "xa2", "xa3"]
     for r in range(NR):
         p = part[r]
         xn, xm = state[r], state[r + 1]
-        for i, (a, b) in enumerate(SP):
-            vtr(T.ps3[:, a // 16:b // 16, :], T.pb[:, 512 * i:512 * i + b - a], [("pb", i, i + 1)], [("ps3", a, b)])
-        vcp(T["sc%d" % r][:], T.ps3[:, :, 0], ["ps3"], ["sc%d" % r])
-        send(p, "a_sc%d" % r, T["tc%d" % r][:], T["sc%d" % r][:], ["sc%d" % r])
-        ld, lds = T["ld%d" % r][:], ["ld%d" % r]
-        lp2, lp3, lps = T["lp%d" % r][:, 0:24], T["lp%d" % r][:, 24:48], ["lp%d" % r]
-        le, les = T["le%d" % r][:], ["le%d" % r]
-        lg2, lg3, lgs = T["lg%d" % r][:, 0:24], T["lg%d" % r][:, 24:48], ["lg%d" % r]
-        for i, (a, b) in enumerate(SP):
-            vtt(T.wo0[:, a:b], T.pb[:, 512 * i:512 * i + b - a], T.tw0[:, a:b], A.max, [("pb", i, i + 1), "tw0"], [("wo0", a, b)])
-        level("v", "wo0", "fo", None, 0, None, None)
-        merge("wo0", "fo", "wo1", ld, lds)
+        ld, tc, sc = a("ld%d" % r), "tc%d" % r, "sc%d" % r
+        more = r + 1 < NR
+
+        def halve(t):
+            act(cols("hx", C * t, C * t + C), a(xn, s_[:, t:4 * C:4]), 0.5)
+
+        for i, (lo, hi) in enumerate(SP):
+            tt(cols("v0t", lo, hi), bank(i, 0, hi - lo), cols("tw0", lo, hi), A.max)
+            tt(cols("v1t", lo, hi), bank(i, 0, hi - lo), cols("tw1", lo, hi), A.max)
+            act(cols("v2t", lo, hi), bank(i, 0, hi - lo), bias=vbias)
+        tt(a("w1"), by(a("v0t"), ld), a("v1t"), A.min)
+        halve(0)
+        tt(a("w2"), by(a("w1"), ld), a("v2t"), A.min)
+        turn(a("po2"), a("w2"))
+        act(a("fo"), a("w2"), bias=fbias)
+        cp(row(sc, 0, 3), row("po2", 1, 4))
+        cp(row(sc, 3, 5), row("po2", 10, 12))
+        send(p, "a_sc%d" % r, a(tc, s_[:, 0:12]), a(sc))
         if r == 0:
-            op("v", lambda q: q.tensor_copy(T.einv[:].indirect(T.le0[:]), T.iota[:]), ["iota", "le0"], ["einv"])
-        send_powers(r)
-        if r == 0:
-            rest_of_constants()
-        for t in range(4):
-            act(T.hx[:, C * t:C * t + C], T[xn][:, t:4 * C:4], [xn], [("hx", C * t, C * t + C)], scale=0.5)
-        if r == 0:
-            act(T.lr[:], T.iota[:].indirect(T.ln[:]), ["iota", "ln"], ["lr"])
-            act(T.lr2[:], T.lr[:].indirect(T.lrho2[:]), ["lr", "lrho2"], ["lr2"])
-            dma("y", "d_n", T.lo[:], T.lr2[0:128:16, :], ["lr2"], ["lo"])
-        level("v", "wo1", "fo", None, 1, None, None)
-        merge("wo1", "fo", "wo0", lp2, lps)
-        level("v", "wo0", "fo", None, 2, None, None)
-        for i in range(6):
-            if i % 2:
-                act(T.kt[:, :, i], T["tc%d" % r][:], ["tc%d" % r], [("kt", 0, 384, i)])
-            else:
-                vcp(T.kt[:, :, i], T["tc%d" % r][:], ["tc%d" % r], [("kt", 0, 384, i)])
-        vtr(T.wt0[:], T.kt[:], ["kt"], ["wt0"])
-        level("s", "wt0", "ft", None, 3, None, None)
-        merge("wo0", "fo", "wo1", lp3, lps)
-        merge("wt0", "ft", "wt1", le, les)
-        level("s", "wt1", "ft", None, 4, None, None)
-        act(T.wo0[:], T.wo1[:], ["wo1", "ct"], ["wo0"], scale=cc(6), bias=cc(7))
-        merge("wt1", "ft", "wt0", lg2, lgs)
-        level("s", "wt0", "ft", None, 5, None, None)
-        vtr(T.po3[:], T.wo0[:], ["wo0"], ["po3"])
-        if r == 0:
-            vcp(T.lnr[:], T.lo[:], ["lo"], ["lnr"])
-            mates_list(0)
-        merge("wt0", "ft", "wt1", lg3, lgs)
-        act(T.base[:, 0:48:2], T.po3[:, :, 8], [("po3", 0, 384, "x")], [("base", 0, 48, 0)])
-        vts(T.vv[:], T.wt1[:].indirect(T.ln[:]), cc(6), cc(8), A.mult, A.add, ["wt1", "ln", "ct"], ["vv"])
-        ss = [("po3", 0, 384, "s")]
-        vtt(T.po3[:, :, 2:6:3], T.po3[:, :, 2:6:3], T.po3[:, :, 1:5:3], A.min, ss, ss)
-        vtt(T.po3[:, :, 4], T.po3[:, :, 4], T.po3[:, :, 2], A.min, ss, ss)
-        vtr(T.pt3[:], T.vv[:], ["vv"], ["pt3"])
-        act(T.base[:, 1:48:2], T.pt3[:, :, 8], [("pt3", 0, 384, "x")], [("base", 0, 48, 1)])
-        ss = [("pt3", 0, 384, "s")]
-        vtt(T.pt3[:, :, 0:4:3], T.pt3[:, :, 0:4:3], T.pt3[:, :, 1:5:3], A.min, ss, ss)
-        vtt(T.pt3[:, :, 1], T.pt3[:, :, 1], T.pt3[:, :, 3], A.min, ss, ss)
-        vtt(T.c6[:], T.po3[:, :, 0:6], T.pt3[:, :, 0:6], A.is_gt, [("po3", 0, 384, "s"), ("pt3", 0, 384, "s")], ["c6"])
-        vtt(T.m6[:, 0:48:2, :], T.c6[:], T.po3[:, :, 9:15], A.mult, ["c6", ("po3", 0, 384, "x")], [("m6", 0, 288, 0)])
-        vtt(T.m6[:, 1:48:2, :], T.c6[:], T.pt3[:, :, 9:15], A.mult, ["c6", ("pt3", 0, 384, "x")], [("m6", 0, 288, 1)])
-        vtt(T.m3[:], T.m6[:, :, 0:3], T.m6[:, :, 3:6], A.max, ["m6"], ["m3"])
-        vtt(T.m1[:], T.m3[:, :, 0], T.m3[:, :, 1], A.max, ["m3"], ["m1"])
-        vtt(T.m2[:], T.m3[:, :, 2], T.base[:], A.max, ["m3", "base"], ["m2"])
-        vtt(T.m0[:], T.m1[:], T.m2[:], A.max, ["m1", "m2"], ["m0"])
-        vts(T.tk[:], T.m0[:], 1.0 / 1024.0, MAGIC, A.mult, A.add, ["m0"], ["tk"])
-        vts(T.m1[:], T.tk[:], -MAGIC, -1024.0, A.add, A.mult, ["tk"], ["m1"])
-        vts(T.ab[:, :, 2], T.tk[:, 0:48:2], -MAGIC, None, A.add, None, ["tk"], [("ab", 0, 72, 1)])
-        vtt(T.ab[:, :, 0:2], T.m0[:], T.m1[:], A.add, ["m0", "m1"], [("ab", 0, 72, 0)])
-        vtt(T.kp[:, :, 0:3], T.ab[:], T.mo[:], A.mult, ["ab", "mo"], [("kp", 0, 384, 0)])
-        act(T.kp[:, :, 3], T.ab[:, :, 2], ["ab"], [("kp", 0, 384, 1)])
-        vtt(T.ai[:], T.ab[:], T.mi[:], A.mult, ["ab", "mi"], ["ai"])
-        vtr(T.rk[:, 16:400], T.kp[:], ["kp"], ["rk"])
-        vtr(T.qk[:], T.rk[:], ["rk"], ["qk"])
-        vtt(T.oab[:], T.ai[:], T.qk[:, 1:25, 0:3], A.add, ["ai", "qk"], ["oab"])
-        vts(T.la[:], T.oab[:, 0:72:3], 192.0, None, A.add, None, ["oab"], ["la"])
-        vts(T.lb[:], T.oab[:, 1:72:3], 192.0, None, A.add, None, ["oab"], ["lb"])
-        vcp(T.knr[:], T.rk[:, 16:400].indirect(T.lnr[:]), ["rk", "lnr"], ["knr"])
-        dma("y", "d_kn%d" % r, T.kno[:], T.knr[3:128:16, :], ["knr"], ["kno"])
-        for i, (a, b) in enumerate(ZP):
+            places_for_partner(0)
+        halve(1)
+        ts(a("fl", s_[:, 0:12, :]), row("po2", 11), 1.0 / ONE, A.mult, -3072.0, A.add)
+        cp(a("fl", s_[:, 12:24, :]), a("le%d" % r))
+        if more:
+            turn(a("ti"), a("ri"))
+            ts(a("fl", s_[:, 24:36, :]), row("ti", 0), MID, A.add)
+        swap1("r5", lambda h: a("fl", s_[:, :, h]))
+        turn(a("tl"), a("rl"))
+        swap2(lambda m: a("ol", s_[:, :, m]), "r5")
+        cp(a("ls%d" % r), row("tl", 0))
+        send(p, "a_lm%d" % r, a("lm%d" % r), a("ls%d" % r))
+        cp(a("l3"), a("ol", s_[:, 0:12, :]))
+        ts(row("kt", 9), a("ol", s_[:, 12:24, :]), 1024.0, A.add, ONE, A.mult)
+        tt(a("w3"), by(a("fo"), a("l3")), a("w2"), A.min)
+        halve(2)
+        halve(3)
+        ts(row("kt", 12), a("ol", s_[:, 12:24, :]), 4096.0 + BIG, A.add, ONE, A.mult)
+        turn(a("po3"), a("w3"))
+        if more:
+            cp(a("li"), a("ol", s_[:, 24:36, :]))
+        tt(row("po3", 4, 6), row("po3", 4, 6), row("po3", 3, 8, 4), A.min)
+        got = lambda lo, hi: a(tc, s_[:, 0:12, :, lo:hi])
+        cp(row("kt", 1, 4), got(0, 3))
+        act(row("kt", 4, 7), got(0, 3))
+        cp(row("kt", 10, 12), got(3, 5))
+        cp(row("kt", 7), got(2, 3))
+        ts(row("kt", 13, 15), got(3, 5), (3072.0 + BIG) * ONE, A.add)
+        swap1("r4a", lambda h: a(tc, s_[:, :, h, 3:5]))
+        for lo, hi in HALF:
+            turn(cols("wt", lo, hi), blocks("kt", lo, hi))
+            if lo == 0:
+                act(cols("ft", lo, hi), cols("wt", lo, hi), bias=fbias)
+                swap2(lambda m: a("oe", s_[:, :, :, m]), "r4a")
+        ts(a("m3"), a("oe", s_[:, 0:12, 1, :]), 1.0 / ONE, A.mult, -3072.0, A.add)
+        ts(cols("ft", 192, C), cols("wt", 192, C), fbias, A.add)
+        tt(a("wu"), by(a("ft"), a("m3")), a("wt"), A.min)
+        act(a("da"), row("po3", 14, 7, -1), 1.0 / ONE)
+        act(a("da", s_[:, 6:168:7]), a("cT"))
+        for e, (lo, hi) in zip("vs", HALF):
+            move(e, cols("vv", lo, hi), by(a("wu"), offs("ln", lo, hi)))
+        for lo, hi in HALF:
+            turn(blocks("pt", lo, hi), cols("vv", lo, hi))
+        tt(row("pt", 4, 6), row("pt", 4, 6), row("pt", 3, 8, 4), A.min)
+        act(a("db"), row("pt", 8, 15), -1.0 / ONE, 8191.0)
+        tt(a("c8"), row("po3", 7, 0, -1), row("pt", 0, 7), A.is_gt)
+        scan(cols("sa", 0, 168), a("c8"), a("da"))
+        scan(cols("sa", 168, 336), a("c8"), a("db"))
+        swap1("r4b", lambda h: a("sa", s_[:, 7 * h + 6:448:14]))
+        cp(a("ki"), a("sa", s_[:, 6:168:7]))
+        swap2(lambda m: a("oa", s_[:, :, m]), "r4b")
+        ts(a("kj"), a("ki"), 10, A.logical_shift_right, 1, A.bitwise_and)
+        cp(a("ni"), a("oa", s_[:, 0:24, :]))
+        cp(row("kp", 4), a("kj"))
+        ts(a("nj"), a("ni"), 1023, A.bitwise_and)
+        cp(row("kp", 5), a("kj"))
+        cp(a("la"), cols("nj", 0, 24))
+        ts(a("lb"), cols("nj", 24, 48), -1.0, A.mult, 1023.0, A.add)
+        cp(row("kp", 6), a("kj"))
+        cp(row("kp", 2), a("lm%d" % r))
+        turn(a("rk"), a("kp"))
+
+        def half_a(lo, hi):
             for t in range(4):
-                act(T.za[:, C * t + a:C * t + b], T.hx[:, C * t:C * t + C].indirect(T.la[:, a // 16:b // 16]),
-                    [("hx", C * t, C * t + C), "la"], [("za", C * t + a, C * t + b)])
-        hq, hqs = T["hq%d" % r], T["hqs%d" % r]
-        for i, (a, b) in enumerate(ZP):
-            for t in range(4):
-                vtt(T.zt[:, 4 * a + t:4 * b:4], T.hx[:, C * t:C * t + C].indirect(T.lb[:, a // 16:b // 16]), T.za[:, C * t + a:C * t + b], A.add,
-                    [("hx", C * t, C * t + C), "lb", ("za", C * t + a, C * t + b)], [("zt", 4 * a, 4 * b, t)])
-            quant(T.zq[:, a:b], T.zqs[:, a:b], T.zt[:, 4 * a:4 * b], [("zt", 4 * a, 4 * b)], [("zq", a, b), ("zqs", a, b)])
+                act(cols("za", C * t + lo, C * t + hi), by(cols("hx", C * t, C * t + C), offs("la", lo, hi)))
+
+        def half_b(lo, hi, planes=range(4)):
+            for t in planes:
+                tt(a("zt", s_[:, 4 * lo + t:4 * hi:4]), by(cols("hx", C * t, C * t + C), offs("lb", lo, hi)), cols("za", C * t + lo, C * t + hi), A.add)
+
+        HQ, HL = ("hq%d" % r, "hqs%d" % r), ("hl%d" % r, "hls%d" % r)
+
+        def layer(i):
+            lo, hi = HP[i]
+            quant(ZQ, lo, hi, cols("zt", 4 * lo, 4 * hi))
             for k in range(4):
-                mm(4 * i + k, b - a, T.wq[:, 128 * k:128 * k + 128], T.wqs[:, 128 * k:128 * k + 128], T.zq[:, a:b], T.zqs[:, a:b],
-                   ["wq", "wqs", ("zq", a, b), ("zqs", a, b)])
+                mm(4 * i + k, WQ, 128 * k, ZQ, lo, hi)
 
-        def hcopy(e, i, k):
-            a, b = HP[i]
-            src = T.pb[:, 512 * (4 * i + k):512 * (4 * i + k) + b - a]
-            rd, wr = [("pb", 4 * i + k, 4 * i + k + 1)], [("ht", 4 * a, 4 * b, k)]
-            if e == "s":
-                act(T.ht[:, 4 * a + k:4 * b:4], src, rd, wr, scale=0.03125)
-            else:
-                vts(T.ht[:, 4 * a + k:4 * b:4], src, 0.03125, None, A.mult, None, rd, wr)
+        def hcopy(i, who):
+            lo, hi = HP[i]
+            for k, e in enumerate(who):
+                move(e, a("ht", s_[:, 4 * lo + k:4 * hi:4]), bank(4 * i + k, 0, hi - lo), 0.03125)
 
-        def hpiece(i):
-            a, b = HP[i]
-            quant(hq[:, a:b], hqs[:, a:b], T.ht[:, 4 * a:4 * b], [("ht", 4 * a, 4 * b)], [("hq%d" % r, a, b), ("hqs%d" % r, a, b)])
+        def hsend(i):
+            lo, hi = HP[i]
+            quant(HQ, lo, hi, cols("ht", 4 * lo, 4 * hi))
             sem = "a_h%d_%d" % (r, i)
-            send(p, sem, T["hl%d" % r][:, a:b].bitcast(dt.uint8), hq[:, a:b].bitcast(dt.uint8), [("hq%d" % r, a, b)])
-            send(p, sem, T["hls%d" % r][:, a:b], hqs[:, a:b], [("hqs%d" % r, a, b)])
+            send(p, sem, raw(cols(HL[0], lo, hi), dt.uint8), raw(cols(HQ[0], lo, hi), dt.uint8))
+            send(p, sem, cols(HL[1], lo, hi), cols(HQ[1], lo, hi))
 
-        for k, e in enumerate("sssv"):
-            hcopy(e, 0, k)
-        hpiece(0)
-        vtt(T.dd[:], T.dno[:], T.fd[:], A.subtract, ["dno", "fd"], ["dd"])
-        vtt(T.kk[:], T.oab[:, 2:72:3], T.kno[:], A.add, ["oab", "kno"], ["kk"])
-        vts(T.kf[:], T.kk[:], 1, None, A.bitwise_and, None, ["kk"], ["kf"])
-        vtt(T.ff[:], T.kf[:], T.dd[:], A.mult, ["kf", "dd"], ["ff"])
-        vtt(T.fd[:], T.ff[:], T.fd[:], A.add, ["ff", "fd"], ["fd"])
-        nl_ = "ld%d" % (r + 1) if r + 1 < NR else "ldf"
-        vcp(T[nl_][:], T.fd[:], ["fd"], [nl_])
-        if r + 1 < NR:
-            send_d(r + 1)
-        for k, e in enumerate("vsvs"):
-            hcopy(e, 1, k)
-        hpiece(1)
+        half_a(*HP[0])
+        half_a(*HP[1])
+        half_b(*HP[0])
+        layer(0)
+        half_b(*HP[1])
+        hcopy(0, "ssss")
+        layer(1)
         if r == 0:
-            quant(T.eq[:], T.eqs[:], T.eb[:], ["eb"], ["eq", "eqs"])
-            quant(T.vq[:], T.vqs[:], T.v0[:], ["v0"], ["vq", "vqs"])
-        act(T.lr[:], T.einv[:].indirect(T[nl_][:]), ["einv", nl_], ["lr"])
-        act(T.lr2[:], T.lr[:].indirect(T.lrho[:, 0:24]), ["lr", ("lrho", 0, 24)], ["lr2"])
-        dma("y", "d_l%d" % r, T.lo[:], T.lr2[0:128:16, :], ["lr2"], ["lo"])
-        a, b = ZP[1]
+            unit(0)
+            unit(1)
+        hsend(0)
+        hcopy(1, "vsvv")
+        act(a("rn"), by(a("rk"), a("ln")))
+        hsend(1)
+        half_a(FAR, C)
+        if r == 0:
+            unit(2)
+            unit(3)
+        turn(a("kn"), a("rn"))
+        tt(a("odd"), row("kp", 4, 7), row("kn", 4, 7), A.not_equal)
+        tt(a("dlt"), row("kn", 1, 4), row("kp", 1, 4), A.subtract)
+        half_b(FAR, C, [0])
+        tt(a("prd"), a("odd"), a("dlt"), A.mult)
+        half_b(FAR, C, [1])
+        tt(a("new", s_[:, 0:12]), a("prd"), row("kp", 1, 4), A.add)
+        half_b(FAR, C, [2])
+        swap1("r4c", lambda h: a("new", s_[:, :, h, 0:2]))
+        half_b(FAR, C, [3])
+        if more:
+            own_tables()
+            act(row("ko", 0), newv(2))
+        swap2(lambda m: a("ob", s_[:, :, :, m]), "r4c")
+        quant(ZO, 0, 128, cols("zt", 4 * (C - 128), 4 * C))
+        nl_ = "ld%d" % (r + 1) if more else "ldf"
+        ts(a(nl_), a("ob", s_[:, 0:12, 0, :]), MID, A.add)
+        ts(a("ll"), a("ob", s_[:, 0:12, 1, :]), MID, A.add)
+        if more:
+            send_d(r + 1)
         for k in range(4):
-            act(T.jt[:, C * k + FAR:C * k + C], T.pb[:, 512 * (4 + k) + FAR - a:512 * (4 + k) + C - a], [("pb", 4 + k, 5 + k)],
-                [("jt", C * k + FAR, C * k + C)], scale=0.03125)
-        if r + 1 < NR:
-            power1(r + 1)
-            op("v", lambda q: q.tensor_copy(T.einv[:].indirect(T["le%d" % (r + 1)][:]), T.iota[:]), ["iota", "le%d" % (r + 1)], ["einv"])
+            mm(k, WQ, 128 * k, ZO, 0, 128)
+        if more:
+            turn(a("tw0"), a("ko"))
+            cp(row("kp", 1), newv(0))
         else:
-            act(T.rt[:, 0:C], T.iota[:].indirect(T.ldf[:]), ["iota", "ldf"], [("rt", 0, C)])
-            dma("y", "out", T.dn[:], T.rt[0:128:16, 0:C], [("rt", 0, C)], [])
-        hl, hls = T["hl%d" % r], T["hls%d" % r]
-        for i, (a, b) in enumerate(HP):
-            for k in range(4):
-                mm(4 * i + k, b - a, T.eq[:, 128 * k:128 * k + 128], T.eqs[:, 128 * k:128 * k + 128], hl[:, a:b], hls[:, a:b],
-                   ["eq", "eqs", ("hl%d" % r, a, b), ("hls%d" % r, a, b)])
+            quant(VQ, 0, 128, a("v0"))
         for k in range(4):
-            for i, (a, b) in enumerate(HP):
-                rd, wr = [("pb", 4 * i + k, 4 * i + k + 1)], [("jt", C * k + a, C * k + b)]
-                src = T.pb[:, 512 * (4 * i + k):512 * (4 * i + k) + b - a]
-                act(T.jt[:, C * k + a:C * k + b], src, rd, wr)
-        vcp(T.ll[:], T.lo[:], ["lo"], ["ll"])
-        for i, (a, b) in enumerate(SP):
+            move("v", cols("jt", C * k + FAR, C * k + C), bank(k, 128 - (C - FAR), 128), 0.03125)
+
+        def unpack(i, b0, who):
+            lo, hi = HP[i]
+            for k in range(4):
+                mm(b0 + k, EQ, 128 * k, HL, lo, hi)
+            for k, e in enumerate(who):
+                move(e, cols("jt", C * k + lo, C * k + hi), bank(b0 + k, 0, hi - lo))
+
+        unpack(0, 4, "ssss")
+        unpack(1, 0, "vsss")
+        if more:
+            act(a("ri"), by(a("tw0"), a("li")))
+            places_for_partner(r + 1)
+        else:
+            act(a("r1"), by(a("iota"), a("ldf")), bias=MID)
+            dma("y", "out", hbm(T.dn[:]), a("r1", s_[0:128:16, :]))
+        for i, (lo, hi) in enumerate(SP):
             for t in range(4):
-                vtt(T[xm][:, 4 * a + t:4 * b:4], T.jt[:, C * t:C * t + C].indirect(T.ll[:, a // 16:b // 16]), T[xn][:, 4 * a + t:4 * b:4], A.add,
-                    [("jt", C * t, C * t + C), "ll", (xn, 4 * a, 4 * b)], [(xm, 4 * a, 4 * b, t)])
-            if r + 1 < NR:
+                tt(a(xm, s_[:, 4 * lo + t:4 * hi:4]), by(cols("jt", C * t, C * t + C), offs("ll", lo, hi)), a(xn, s_[:, 4 * lo + t:4 * hi:4]), A.add)
+            if more:
                 score(xm, i)
             else:
-                quant(T.xq[:, a:b], T.xqs[:, a:b], T[xm][:, 4 * a:4 * b], [(xm, 4 * a, 4 * b)], [("xq", a, b), ("xqs", a, b)])
-        if r + 1 < NR:
-            powers2(r + 1)
-            mates_list(r + 1)
-    dma("y", "out", T.oc[:], T.xq[:].bitcast(dt.uint8), ["xq"], [])
+                quant(XQ, lo, hi, cols(xm, 4 * lo, 4 * hi))
+                mm(4 + i, VQ, 0, XQ, lo, hi)
+                dma("y", "out", hbm(T.oc[:, 4 * lo:4 * hi]), raw(cols("xq", lo, hi), dt.uint8))
+                move("sv"[i], cols("ysb", lo, hi), bank(4 + i, 0, hi - lo))
+                dma("s", "out", hbm(T.y[:, lo:hi]), cols("ysb", lo, hi))
     for k in range(4):
-        dma("y", "out", T.osc[4 * k:4 * k + 4, :], T.xqs[32 * k:32 * k + 4, :], ["xqs"], [])
-    for i in range(2):
-        mm(i, 192, T.vq[:], T.vqs[:], T.xq[:, 192 * i:192 * i + 192], T.xqs[:, 192 * i:192 * i + 192], ["vq", "vqs", "xq", "xqs"])
-    act(T.ysb[:, 0:192], T.pb[:, 0:192], [("pb", 0, 1)], [("ysb", 0, 192)])
-    vcp(T.ysb[:, 192:384], T.pb[:, 512:704], [("pb", 1, 2)], [("ysb", 192, 384)])
-    dma("y", "out", T.y[:], T.ysb[:], ["ysb"], [])
+        dma("y", "out", hbm(T.osc[4 * k:4 * k + 4, :]), a("xqs", s_[32 * k:32 * k + 4, :]))
     for s, v in total.items():
         need("g", (s, v))

@@ -20,40 +20,41 @@ def declare(dtype, shape, names, where="sbuf"):
         SCRATCH[name] = (where, [128] + shape, dtype)
 
 
-declare("bfloat16", [4 * C], "x0 xa1 xa2 xa3 hx za zt jt")
+declare("bfloat16", [4 * C], "x0 xa1 xa2 hx za zt jt")
 declare("bfloat16", [4 * FAR], "ht")
-declare("bfloat16", [512], "u0 v0")
+declare("bfloat16", [512], "u0 v0 jg")
 declare("bfloat16", [516], "ones dg")
 declare("bfloat16", [24, 16], "kp kn ti tl")
 declare("bfloat16", [C], "rk rn ri rl")
 declare("float32", [4096], "pb", "psum")
-declare("int32", [24], "dli nli ki kj")
+declare("int32", [24], "dli nli ni nj")
 declare("int32", [8], "iu")
-declare("int32", [48], "ni nj")
+declare("int32", [48], "nk")
 declare("uint16", [8], "lu")
-declare("uint16", [24], "ln la lb ll l3 m3 li ldf")
-declare("float32", [24, 16], "ko k1 kt po2 po3 pt")
-declare("float32", [2, 2, 16], "vt")
+declare("uint16", [24], "ln la lb ll li ldf")
+declare("float32", [24, 16], "ko k1 po2 po3 pt")
+declare("float32", [16, 2, 16], "kt")
+declare("float32", [2, 2, 16], "vt r4a r4b")
 declare("float32", [64], "ct")
-declare("float32", [24], "cT")
-declare("float32", [C], "iota tw0 tw1 v0t v1t v2t w1 w2 w3 fo wt ft wu vv r1 ysb")
+declare("float32", [24], "cT odd")
+declare("float32", [C], "iota tw0 tw1 v0t v1t v2t w1 w2 fo wt ft wu vv ysb")
 declare("float32", [168], "c8 da db")
-declare("float32", [24, 3], "odd dlt prd")
+declare("float32", [24, 3], "dlt prd")
 declare("float32", [448], "sa")
-declare("float32", [16, 2, 3], "new")
-declare("float32", [64, 2], "fl ol")
+declare("float32", [24, 7], "dd")
+declare("float32", [16, 2, 4], "new")
+declare("float32", [32, 2], "fl ol oa")
 declare("float32", [4, 2, 16], "r5")
-declare("float32", [2, 2, 16], "r4a r4b r4c")
-declare("float32", [32, 2], "oa")
-declare("float32", [16, 2, 2], "ob oe")
+declare("float32", [16, 2, 2], "oe")
+declare("float32", [16, 4, 2], "ob")
 for _n, _w in (("uq", 128), ("ur", 128), ("vq", 128), ("wq", 512), ("eq", 512), ("xq", C), ("zq", FAR), ("zo", 128)):
     declare("float8_e4m3fn_x4", [_w], _n)
     declare("uint8", [_w], _n + "s")
-SEMAPHORES = ["cv", "cs", "ct", "cg", "loc", "out"] + ["ld_" + k for k in ("x0", "x1", "u", "v", "wc", "wsp", "dl", "nl")]
+SEMAPHORES = ["cv", "cs", "ct", "cg", "loc", "out", "hand0", "hand1"]
+SEMAPHORES += ["ld_" + k for k in ("x0", "x1", "u", "v", "wc", "wsp", "dl", "nl")]
 for _r in range(NR):
-    declare("float32", [24, 5], "sc%d" % _r)
-    declare("float32", [16, 2, 5], "tc%d" % _r)
-    declare("uint16", [24], "ld%d le%d" % (_r, _r))
+    declare("float32", [24, 5], "sc%d tc%d" % (_r, _r))
+    declare("uint16", [24], "ld%d le%d l3%d m3%d" % (_r, _r, _r, _r))
     declare("bfloat16", [24], "ls%d lm%d" % (_r, _r))
     for _k in ("hq", "hl"):
         declare("float8_e4m3fn_x4", [FAR], "%s%d" % (_k, _r))
@@ -62,9 +63,35 @@ for _r in range(NR):
     SEMAPHORES += ["a_h%d_%d" % (_r, p) for p in range(len(HP))]
 
 
+def helpers(T, topo):
+    via = {}
+    for c in T.cores:
+        p = T.cores[T.rank_of(c) ^ MASKS[NR - 1]]
+        same = [k for k in T.cores if topo.chip(k) == topo.chip(c) and topo.die(k) == topo.die(c)]
+        free = [k for k in topo.cores_of(c) if k not in T.cores and k not in via.values() and topo.die(k) != topo.die(c) and topo.may_write(k, p)]
+        if topo.chip(c) != topo.chip(p) and same.index(c) % 2 and free:
+            via[c] = free[0]
+    return via
+
+
+def hand_on(g, core, T, topo, src):
+    r = NR - 1
+    dst = T.cores[T.rank_of(src) ^ MASKS[r]]
+    lo, hi = HP[0]
+    rid, pid, _ = topo.addr(dst)
+    for k, piece in enumerate((T["hl%d" % r][:, lo:hi].bitcast(dt.uint8), T["hls%d" % r][:, lo:hi])):
+        g.wait_ge(T.sem["hand%d" % k], len(topo.engines(src, core)))
+        g.remote_dma(piece, piece, T.sem["a_h%d_0" % r], T.sem["loc"], pid, rid, topo.mask(core, dst))
+    g.wait_ge(T.sem["loc"], 2 * len(topo.engines(core, dst)))
+
+
 def rank_program(g, core, T, topo):
     rank = T.rank_of(core)
+    via = helpers(T, topo)
     if rank is None:
+        for src, k in via.items():
+            if k == core:
+                hand_on(g, core, T, topo, src)
         return
     que = {"v": g.vector, "s": g.scalar, "t": g.tensor, "g": g, "y": g.sync}
     total, know, recs = {}, {}, {}
@@ -152,11 +179,12 @@ def rank_program(g, core, T, topo):
 
     part = [T.cores[rank ^ m] for m in MASKS]
     for r in range(NR):
-        lands(part[r], "a_sc%d" % r, [a("tc%d" % r, s_[:, 0:12])])
+        lands(part[r], "a_sc%d" % r, [a("tc%d" % r)])
         lands(part[r], "a_le%d" % r, [a("le%d" % r)])
         lands(part[r], "a_lm%d" % r, [a("lm%d" % r)])
         for i, (lo, hi) in enumerate(HP):
-            lands(part[r], "a_h%d_%d" % (r, i), [cols("hl%d" % r, lo, hi), cols("hls%d" % r, lo, hi)])
+            src = via.get(part[r], part[r]) if (r, i) == (NR - 1, 0) else part[r]
+            lands(src, "a_h%d_%d" % (r, i), [cols("hl%d" % r, lo, hi), cols("hls%d" % r, lo, hi)])
 
     def val(x):
         return x[0] if isinstance(x, tuple) else x
@@ -179,8 +207,8 @@ def rank_program(g, core, T, topo):
     def turn(out, in_):
         op("v", lambda q: q.transpose(out[0], in_[0]), [in_], [out])
 
-    def scan(out, d0, d1):
-        op("v", lambda q: q.tensor_tensor_scan(out[0], d0[0], d1[0], 0.0, A.mult, A.max), [d0, d1], [out])
+    def scan(out, d0, d1, o):
+        op("v", lambda q: q.tensor_tensor_scan(out[0], d0[0], d1[0], 0.0, A.mult, o), [d0, d1], [out])
 
     def act(out, in_, scale=None, bias=None):
         if bias is not None:
@@ -217,10 +245,11 @@ def rank_program(g, core, T, topo):
             op("g", lambda q: q.iota(out[0], pattern, base, cm), [], [out])
 
     def row(name, lo, hi=None, step=1):
-        return a(name, s_[:, :, lo] if hi is None else s_[:, :, lo:hi:step])
+        at = lo if hi is None else slice(lo, hi, step)
+        return a(name, s_[:, 0:12, :, at] if name == "kt" else s_[:, :, at])
 
     def blocks(name, lo, hi):
-        return a(name, s_[:, lo // 16:hi // 16, :])
+        return a(name, s_[:, lo // 32:hi // 32] if name == "kt" else s_[:, lo // 16:hi // 16, :])
 
     def offs(name, lo, hi):
         return cols(name, lo // 16, hi // 16)
@@ -240,7 +269,8 @@ def rank_program(g, core, T, topo):
     dma("s", "ld_u", a("u0"), hbm(T.u[:]))
     for i, (lo, hi) in enumerate(SP):
         dma("ys"[i], "ld_x%d" % i, cols("x0", 4 * lo, 4 * hi), hbm(T.x[:, 4 * lo:4 * hi]))
-    dma("s", "ld_nl", a("nli"), hbm(T.nl[:]))
+    need("y", ("ld_x0", 16))
+    dma("y", "ld_nl", a("nli"), hbm(T.nl[:]))
     dma("y", "ld_wc", raw(a("wq"), dt.uint8), hbm(T.wc[:]))
     dma("y", "ld_wsp", a("wqs"), hbm(T.ws[:]))
     dma("y", "ld_v", a("v0"), hbm(T.v[:]))
@@ -251,29 +281,29 @@ def rank_program(g, core, T, topo):
     iota(a("iu"), [[16, 8]], 0, 0)
     iota(a("iota"), [[1, C]], -int(MID), 0, True)
     op("g", lambda q: q.affine_select(T.dg[:], T.ones[:], [[-1, 516]], A.is_equal, 0.0, 3, 4), [a("ones")], [a("dg")])
-    for name in ("vt", "ko", "k1"):
-        fill(a(name), HUGE)
+    for name, c in (("k1", HUGE), ("ko", HUGE), ("kp", 0.0)):
+        act(a(name), cols("ones", 0, C), c)
+    fill(a("vt"), HUGE)
     fill(a("vt", s_[:, 0, :, 4:7]), 0.0)
     fill(a("vt", s_[:, 0, :, 12:15]), -BIG * ONE)
     fill(a("vt", s_[:, 1, :, 1:8]), 0.0)
-    for name, lo, hi in (("k1", 2, 4), ("k1", 5, 8), ("ko", 3, 4), ("ko", 6, 8)):
-        fill(row(name, lo, hi), -HUGE)
-    for name, r_, k in (("k1", 9, 1024.0), ("k1", 12, 4096.0 + BIG), ("ko", 10, 2048.0), ("ko", 13, 5120.0 + BIG), ("kt", 8, 0.0)):
-        ts(row(name, r_), a("cT"), k, A.add, ONE, A.mult)
+    fill(row("kt", 0, 16, 15), HUGE)
+    fill(cols("sa", 336, 448), 0.0)
+    fill(a("new"), 0.0)
+    fill(a("fl"), 0.0)
+    fill(a("kt", s_[:, 12:16, :, 10:12]), 0.0)
     turn(a("ct"), a("vt"))
+    for name, runs, places in (("k1", ((2, 4), (5, 8)), ((9, 1024.0), (12, 4096.0 + BIG))), ("ko", ((3, 4), (6, 8)), ((10, 2048.0), (13, 5120.0 + BIG)))):
+        for lo, hi in runs:
+            fill(row(name, lo, hi), -HUGE)
+        for r_, k in places:
+            ts(row(name, r_), a("cT"), k, A.add, ONE, A.mult)
+        if name == "k1":
+            turn(a("tw1"), a("k1"))
+    ts(row("kt", 8), a("cT"), ONE, A.mult)
     cp(a("lu"), a("iu"))
-    turn(a("tw1"), a("k1"))
-    fill(a("kp"), 0.0)
-
-    def small_constants():
-        fill(row("kt", 0, 16, 15), HUGE)
-        fill(cols("sa", 336, 448), 0.0)
-        fill(a("new", s_[:, 12:16]), 0.0)
-        fill(a("fl", s_[:, 36:64, :]), 0.0)
-        ts(row("kp", 3), a("cT"), -MID, A.add)
-
-    for r in range(NR):
-        fill(a("tc%d" % r, s_[:, 12:16]), 0.0)
+    ts(row("kp", 3), a("cT"), -MID, A.add)
+    ts(row("dd", 6), a("cT"), 1024.0, A.add, ONE, A.mult)
 
     def newv(k):
         return a("new", s_[:, 0:12, :, k])
@@ -288,9 +318,6 @@ def rank_program(g, core, T, topo):
     def places_for_partner(r):
         act(a("rl"), by(a("ri"), a("le%d" % r)))
 
-    def unit(b):
-        quant(EQ, 128 * b, 128 * b + 128, cols("dg", 3 - b, 515 - b))
-
     def score(xn, i):
         lo, hi = SP[i]
         quant(XQ, lo, hi, cols(xn, 4 * lo, 4 * hi))
@@ -298,30 +325,34 @@ def rank_program(g, core, T, topo):
 
     cp(a("ld0"), a("dli"))
     send_d(0)
-    act(a("r1"), by(a("iota"), a("ld0")))
+    ts(a("fl", s_[:, 0:12, :]), a("dli"), -MID, A.add)
     quant(UQ, 0, 128, a("u0"))
+    swap1("r4a", lambda h: a("fl", s_[:, :, h]))
     cp(raw(a("ur"), dt.uint32), by(raw(a("uq"), dt.uint32), a("lu")))
     act(a("urs"), by(a("uqs"), a("lu")))
-    small_constants()
-    turn(a("po3"), a("r1"))
-    cp(newv(0), row("po3", 0))
+    swap2(lambda m: a("ol", s_[:, :, m]), "r4a")
+    cp(newv(0), a("ol", s_[:, 0:12, :]))
     own_tables()
     act(row("kp", 1), newv(0))
     cp(by(a("ri"), a("ld0")), a("iota"))
     score("x0", 0)
     turn(a("tw0"), a("ko"))
     score("x0", 1)
-    cp(a("ln"), a("nli"))
 
-    state = ["x0", "xa1", "xa2", "xa3"]
+    state = ["x0", "xa1", "xa2", "xa1"]
     for r in range(NR):
         p = part[r]
         xn, xm = state[r], state[r + 1]
         ld, tc, sc = a("ld%d" % r), "tc%d" % r, "sc%d" % r
+        l3, m3 = a("l3%d" % r), a("m3%d" % r)
         more = r + 1 < NR
 
         def halve(t):
             act(cols("hx", C * t, C * t + C), a(xn, s_[:, t:4 * C:4]), 0.5)
+
+        def send_places():
+            act(a("ls%d" % r), row("tl", 0))
+            send(p, "a_lm%d" % r, a("lm%d" % r), a("ls%d" % r))
 
         for i, (lo, hi) in enumerate(SP):
             tt(cols("v0t", lo, hi), bank(i, 0, hi - lo), cols("tw0", lo, hi), A.max)
@@ -332,49 +363,52 @@ def rank_program(g, core, T, topo):
         tt(a("w2"), by(a("w1"), ld), a("v2t"), A.min)
         turn(a("po2"), a("w2"))
         act(a("fo"), a("w2"), bias=fbias)
-        cp(row(sc, 0, 3), row("po2", 1, 4))
         cp(row(sc, 3, 5), row("po2", 10, 12))
-        send(p, "a_sc%d" % r, a(tc, s_[:, 0:12]), a(sc))
+        cp(row(sc, 0, 3), row("po2", 1, 4))
+        send(p, "a_sc%d" % r, a(tc), a(sc))
         if r == 0:
             places_for_partner(0)
         halve(1)
         ts(a("fl", s_[:, 0:12, :]), row("po2", 11), 1.0 / ONE, A.mult, -3072.0, A.add)
         cp(a("fl", s_[:, 12:24, :]), a("le%d" % r))
-        if more:
-            turn(a("ti"), a("ri"))
-            ts(a("fl", s_[:, 24:36, :]), row("ti", 0), MID, A.add)
-        swap1("r5", lambda h: a("fl", s_[:, :, h]))
-        turn(a("tl"), a("rl"))
-        swap2(lambda m: a("ol", s_[:, :, m]), "r5")
-        cp(a("ls%d" % r), row("tl", 0))
-        send(p, "a_lm%d" % r, a("lm%d" % r), a("ls%d" % r))
-        cp(a("l3"), a("ol", s_[:, 0:12, :]))
-        ts(row("kt", 9), a("ol", s_[:, 12:24, :]), 1024.0, A.add, ONE, A.mult)
-        tt(a("w3"), by(a("fo"), a("l3")), a("w2"), A.min)
+        swap1("r4a", lambda h: a("fl", s_[:, :, h]))
+        if r:
+            turn(a("tl"), a("rl"))
+        swap2(lambda m: a("ol", s_[:, :, m]), "r4a")
+        cp(l3, a("ol", s_[:, 0:12, :]))
+        if r:
+            send_places()
+        act(row("kt", 9), a("ol", s_[:, 12:24, :]), ONE, 1024.0 * ONE)
+        act(row("kt", 12), a("ol", s_[:, 12:24, :]), ONE, (4096.0 + BIG) * ONE)
+        tt(a("w1"), by(a("fo"), l3), a("w2"), A.min)
         halve(2)
         halve(3)
-        ts(row("kt", 12), a("ol", s_[:, 12:24, :]), 4096.0 + BIG, A.add, ONE, A.mult)
-        turn(a("po3"), a("w3"))
-        if more:
-            cp(a("li"), a("ol", s_[:, 24:36, :]))
+        if r == 0:
+            turn(a("tl"), a("rl"))
+            send_places()
+            cp(a("ln"), a("nli"))
+        turn(a("po3"), a("w1"))
+        ts(row("po3", 8), a("cT"), ONE, A.mult)
         tt(row("po3", 4, 6), row("po3", 4, 6), row("po3", 3, 8, 4), A.min)
-        got = lambda lo, hi: a(tc, s_[:, 0:12, :, lo:hi])
-        cp(row("kt", 1, 4), got(0, 3))
-        act(row("kt", 4, 7), got(0, 3))
-        cp(row("kt", 10, 12), got(3, 5))
-        cp(row("kt", 7), got(2, 3))
-        ts(row("kt", 13, 15), got(3, 5), (3072.0 + BIG) * ONE, A.add)
-        swap1("r4a", lambda h: a(tc, s_[:, :, h, 3:5]))
+        tt(row("dd", 0, 6), row("po3", 14, 8, -1), row("po3", 13, 7, -1), A.subtract)
+        if more:
+            turn(a("ti"), a("ri"))
+            cp(newv(3), row("ti", 0))
+        act(row("kt", 4, 7), row(tc, 0, 3))
+        cp(row("kt", 10, 12), row(tc, 3, 5))
+        cp(row("kt", 1, 4), row(tc, 0, 3))
+        cp(row("kt", 7), row(tc, 2))
+        ts(row("kt", 13, 15), row(tc, 3, 5), (3072.0 + BIG) * ONE, A.add)
+        swap1("r4a", lambda h: a("kt", s_[:, :, h, 10:12]))
         for lo, hi in HALF:
             turn(cols("wt", lo, hi), blocks("kt", lo, hi))
             if lo == 0:
                 act(cols("ft", lo, hi), cols("wt", lo, hi), bias=fbias)
                 swap2(lambda m: a("oe", s_[:, :, :, m]), "r4a")
-        ts(a("m3"), a("oe", s_[:, 0:12, 1, :]), 1.0 / ONE, A.mult, -3072.0, A.add)
+        ts(m3, a("oe", s_[:, 0:12, 1, :]), 1.0 / ONE, A.mult, -3072.0, A.add)
         ts(cols("ft", 192, C), cols("wt", 192, C), fbias, A.add)
-        tt(a("wu"), by(a("ft"), a("m3")), a("wt"), A.min)
-        act(a("da"), row("po3", 14, 7, -1), 1.0 / ONE)
-        act(a("da", s_[:, 6:168:7]), a("cT"))
+        tt(a("wu"), by(a("ft"), m3), a("wt"), A.min)
+        act(a("da"), a("dd"), 1.0 / ONE, -1024.0)
         for e, (lo, hi) in zip("vs", HALF):
             move(e, cols("vv", lo, hi), by(a("wu"), offs("ln", lo, hi)))
         for lo, hi in HALF:
@@ -382,19 +416,17 @@ def rank_program(g, core, T, topo):
         tt(row("pt", 4, 6), row("pt", 4, 6), row("pt", 3, 8, 4), A.min)
         act(a("db"), row("pt", 8, 15), -1.0 / ONE, 8191.0)
         tt(a("c8"), row("po3", 7, 0, -1), row("pt", 0, 7), A.is_gt)
-        scan(cols("sa", 0, 168), a("c8"), a("da"))
-        scan(cols("sa", 168, 336), a("c8"), a("db"))
+        scan(cols("sa", 0, 168), a("c8"), a("da"), A.add)
+        scan(cols("sa", 168, 336), a("c8"), a("db"), A.max)
         swap1("r4b", lambda h: a("sa", s_[:, 7 * h + 6:448:14]))
-        cp(a("ki"), a("sa", s_[:, 6:168:7]))
+        cp(cols("nk", 0, 24), a("sa", s_[:, 174:336:7]))
         swap2(lambda m: a("oa", s_[:, :, m]), "r4b")
-        ts(a("kj"), a("ki"), 10, A.logical_shift_right, 1, A.bitwise_and)
-        cp(a("ni"), a("oa", s_[:, 0:24, :]))
-        cp(row("kp", 4), a("kj"))
+        cp(a("la"), a("oa", s_[:, 0:12, :]))
+        cp(a("ni"), a("oa", s_[:, 12:24, :]))
+        ts(cols("nk", 24, 48), cols("nk", 0, 24), 10, A.logical_shift_right, 1, A.bitwise_and)
         ts(a("nj"), a("ni"), 1023, A.bitwise_and)
-        cp(row("kp", 5), a("kj"))
-        cp(a("la"), cols("nj", 0, 24))
-        ts(a("lb"), cols("nj", 24, 48), -1.0, A.mult, 1023.0, A.add)
-        cp(row("kp", 6), a("kj"))
+        cp(row("kp", 4), cols("nk", 24, 48))
+        ts(a("lb"), a("nj"), -1.0, A.mult, 1023.0, A.add)
         cp(row("kp", 2), a("lm%d" % r))
         turn(a("rk"), a("kp"))
 
@@ -402,8 +434,8 @@ def rank_program(g, core, T, topo):
             for t in range(4):
                 act(cols("za", C * t + lo, C * t + hi), by(cols("hx", C * t, C * t + C), offs("la", lo, hi)))
 
-        def half_b(lo, hi, planes=range(4)):
-            for t in planes:
+        def half_b(lo, hi):
+            for t in range(4):
                 tt(a("zt", s_[:, 4 * lo + t:4 * hi:4]), by(cols("hx", C * t, C * t + C), offs("lb", lo, hi)), cols("za", C * t + lo, C * t + hi), A.add)
 
         HQ, HL = ("hq%d" % r, "hqs%d" % r), ("hl%d" % r, "hls%d" % r)
@@ -422,57 +454,62 @@ def rank_program(g, core, T, topo):
         def hsend(i):
             lo, hi = HP[i]
             quant(HQ, lo, hi, cols("ht", 4 * lo, 4 * hi))
-            sem = "a_h%d_%d" % (r, i)
-            send(p, sem, raw(cols(HL[0], lo, hi), dt.uint8), raw(cols(HQ[0], lo, hi), dt.uint8))
-            send(p, sem, cols(HL[1], lo, hi), cols(HQ[1], lo, hi))
+            around = i == 0 and not more and core in via
+            to, sems = (via[core], ("hand0", "hand1")) if around else (p, ("a_h%d_%d" % (r, i),) * 2)
+            send(to, sems[0], raw(cols(HL[0], lo, hi), dt.uint8), raw(cols(HQ[0], lo, hi), dt.uint8))
+            send(to, sems[1], cols(HL[1], lo, hi), cols(HQ[1], lo, hi))
 
         half_a(*HP[0])
         half_a(*HP[1])
         half_b(*HP[0])
         layer(0)
         half_b(*HP[1])
-        hcopy(0, "ssss")
         layer(1)
-        if r == 0:
-            unit(0)
-            unit(1)
+        hcopy(0, "sssv")
         hsend(0)
         hcopy(1, "vsvv")
+        half_a(FAR, C)
         act(a("rn"), by(a("rk"), a("ln")))
         hsend(1)
-        half_a(FAR, C)
+        half_b(FAR, C)
+        quant(ZO, 0, 128, cols("zt", 4 * (C - 128), 4 * C))
+        for k in range(4):
+            mm(k, WQ, 128 * k, ZO, 0, 128)
         if r == 0:
-            unit(2)
-            unit(3)
+            for b in range(4):
+                quant(EQ, 128 * b, 128 * b + 128, cols("dg", 3 - b, 515 - b))
+
+        def own_columns(k):
+            move("v", cols("jt", C * k + FAR, C * k + C), bank(k, 128 - (C - FAR), 128), 0.03125)
+
+        kinds = 3 if more else 2
         turn(a("kn"), a("rn"))
-        tt(a("odd"), row("kp", 4, 7), row("kn", 4, 7), A.not_equal)
-        tt(a("dlt"), row("kn", 1, 4), row("kp", 1, 4), A.subtract)
-        half_b(FAR, C, [0])
-        tt(a("prd"), a("odd"), a("dlt"), A.mult)
-        half_b(FAR, C, [1])
-        tt(a("new", s_[:, 0:12]), a("prd"), row("kp", 1, 4), A.add)
-        half_b(FAR, C, [2])
-        swap1("r4c", lambda h: a("new", s_[:, :, h, 0:2]))
-        half_b(FAR, C, [3])
+        own_columns(0)
+        tt(a("odd"), row("kp", 4), row("kn", 4), A.not_equal)
+        tt(row("dlt", 0, kinds), row("kn", 1, 1 + kinds), row("kp", 1, 1 + kinds), A.subtract)
+        own_columns(1)
+        for k in range(kinds):
+            tt(row("prd", k), a("odd"), row("dlt", k), A.mult)
+        own_columns(2)
+        tt(a("new", s_[:, 0:12, :, 0:kinds]), row("prd", 0, kinds), row("kp", 1, 1 + kinds), A.add)
+        own_columns(3)
+        swap1("r5", lambda h: a("new", s_[:, :, h, :]))
         if more:
             own_tables()
             act(row("ko", 0), newv(2))
-        swap2(lambda m: a("ob", s_[:, :, :, m]), "r4c")
-        quant(ZO, 0, 128, cols("zt", 4 * (C - 128), 4 * C))
+            cp(row("kp", 1), newv(0))
+        swap2(lambda m: a("ob", s_[:, :, :, m]), "r5")
         nl_ = "ld%d" % (r + 1) if more else "ldf"
         ts(a(nl_), a("ob", s_[:, 0:12, 0, :]), MID, A.add)
         ts(a("ll"), a("ob", s_[:, 0:12, 1, :]), MID, A.add)
         if more:
             send_d(r + 1)
-        for k in range(4):
-            mm(k, WQ, 128 * k, ZO, 0, 128)
-        if more:
+            ts(a("li"), a("ob", s_[:, 0:12, 3, :]), MID, A.add)
             turn(a("tw0"), a("ko"))
-            cp(row("kp", 1), newv(0))
         else:
             quant(VQ, 0, 128, a("v0"))
-        for k in range(4):
-            move("v", cols("jt", C * k + FAR, C * k + C), bank(k, 128 - (C - FAR), 128), 0.03125)
+            act(a("v0t"), by(a("iota"), a("ldf")), bias=MID)
+            dma("y", "out", hbm(T.dn[:]), a("v0t", s_[0:128:16, :]))
 
         def unpack(i, b0, who):
             lo, hi = HP[i]
@@ -481,26 +518,31 @@ def rank_program(g, core, T, topo):
             for k, e in enumerate(who):
                 move(e, cols("jt", C * k + lo, C * k + hi), bank(b0 + k, 0, hi - lo))
 
-        unpack(0, 4, "ssss")
-        unpack(1, 0, "vsss")
+        late = 0 if not more and p in via else 1
+        unpack(1 - late, 4, "ssss" if more else "vsvs")
+        unpack(late, 0, "vsss")
+        lo, hi = SP[1]
+        for t in range(4):
+            act(a("jg", s_[:, t:4 * (hi - lo):4]), by(cols("jt", C * t, C * t + C), offs("ll", lo, hi)))
         if more:
             act(a("ri"), by(a("tw0"), a("li")))
             places_for_partner(r + 1)
-        else:
-            act(a("r1"), by(a("iota"), a("ldf")), bias=MID)
-            dma("y", "out", hbm(T.dn[:]), a("r1", s_[0:128:16, :]))
         for i, (lo, hi) in enumerate(SP):
-            for t in range(4):
-                tt(a(xm, s_[:, 4 * lo + t:4 * hi:4]), by(cols("jt", C * t, C * t + C), offs("ll", lo, hi)), a(xn, s_[:, 4 * lo + t:4 * hi:4]), A.add)
+            if i == 0:
+                for t in range(4):
+                    tt(a(xm, s_[:, 4 * lo + t:4 * hi:4]), by(cols("jt", C * t, C * t + C), offs("ll", lo, hi)), a(xn, s_[:, 4 * lo + t:4 * hi:4]), A.add)
+            else:
+                tt(cols(xm, 4 * lo, 4 * hi), a("jg"), cols(xn, 4 * lo, 4 * hi), A.add)
             if more:
                 score(xm, i)
             else:
                 quant(XQ, lo, hi, cols(xm, 4 * lo, 4 * hi))
                 mm(4 + i, VQ, 0, XQ, lo, hi)
                 dma("y", "out", hbm(T.oc[:, 4 * lo:4 * hi]), raw(cols("xq", lo, hi), dt.uint8))
+                if i:
+                    for k in range(4):
+                        dma("ys"[k % 2], "out", hbm(T.osc[4 * k:4 * k + 4, :]), a("xqs", s_[32 * k:32 * k + 4, :]))
                 move("sv"[i], cols("ysb", lo, hi), bank(4 + i, 0, hi - lo))
                 dma("s", "out", hbm(T.y[:, lo:hi]), cols("ysb", lo, hi))
-    for k in range(4):
-        dma("y", "out", hbm(T.osc[4 * k:4 * k + 4, :]), a("xqs", s_[32 * k:32 * k + 4, :]))
     for s, v in total.items():
         need("g", (s, v))

import numpy as np
from concourse.mybir import AluOpType as A, ActivationFunctionType as F, dt

C, FAR, NR = 384, 288, 3
MASKS = [1, 2, 4]
HP = [(0, 160), (160, 288)]
SP = [(0, 256), (256, 384)]
HALF = [(0, 192), (192, 384)]
HUGE = 1e29
ONE = 2.0 ** 80
BIG = 8192.0
MID = 192.0
s_ = np.s_

SCRATCH = {}


def declare(dtype, shape, names, where="sbuf"):
    for name in names.split():
        SCRATCH[name] = (where, [128] + shape, dtype)


declare("bfloat16", [4 * C], "x0 xa1 xa2 hx za zt jt")
declare("bfloat16", [4 * FAR], "ht")
declare("bfloat16", [512], "u0 v0 jg")
declare("bfloat16", [516], "ones dg")
declare("bfloat16", [24, 16], "kp kn ti tl")
declare("bfloat16", [C], "rk rn ri rl")
declare("float32", [4096], "pb", "psum")
declare("int32", [24], "dli nli ni nj")
declare("int32", [8], "iu")
declare("int32", [48], "nk")
declare("uint16", [8], "lu")
declare("uint16", [24], "ln la lb ll li ldf")
declare("float32", [24, 16], "ko k1 po2 po3 pt")
declare("float32", [16, 2, 16], "kt")
declare("float32", [2, 2, 16], "vt r4a r4b")
declare("float32", [64], "ct")
declare("float32", [24], "cT odd")
declare("float32", [C], "iota tw0 tw1 v0t v1t v2t w1 w2 fo wt ft wu vv ysb")
declare("float32", [168], "c8 da db")
declare("float32", [24, 3], "dlt prd")
declare("float32", [448], "sa")
declare("float32", [24, 7], "dd")
declare("float32", [16, 2, 4], "new")
declare("float32", [32, 2], "fl ol oa")
declare("float32", [4, 2, 16], "r5")
declare("float32", [16, 2, 2], "oe")
declare("float32", [16, 4, 2], "ob")
for _n, _w in (("uq", 128), ("ur", 128), ("vq", 128), ("wq", 512), ("eq", 512), ("xq", C), ("zq", FAR), ("zo", 128)):
    declare("float8_e4m3fn_x4", [_w], _n)
    declare("uint8", [_w], _n + "s")
SEMAPHORES = ["cv", "cs", "ct", "cg", "loc", "out", "hand0", "hand1"]
SEMAPHORES += ["ld_" + k for k in ("x0", "x1", "u", "v", "wc", "wsp", "dl", "nl")]
for _r in range(NR):
    declare("float32", [24, 5], "sc%d tc%d" % (_r, _r))
    declare("uint16", [24], "ld%d le%d l3%d m3%d" % (_r, _r, _r, _r))
    declare("bfloat16", [24], "ls%d lm%d" % (_r, _r))
    for _k in ("hq", "hl"):
        declare("float8_e4m3fn_x4", [FAR], "%s%d" % (_k, _r))
        declare("uint8", [FAR], "%ss%d" % (_k, _r))
    SEMAPHORES += [k + str(_r) for k in ("a_sc", "a_le", "a_lm")]
    SEMAPHORES += ["a_h%d_%d" % (_r, p) for p in range(len(HP))]


def helpers(T, topo):
    via = {}
    for c in T.cores:
        p = T.cores[T.rank_of(c) ^ MASKS[NR - 1]]
        same = [k for k in T.cores if topo.chip(k) == topo.chip(c) and topo.die(k) == topo.die(c)]
        free = [k for k in topo.cores_of(c) if k not in T.cores and k not in via.values() and topo.die(k) != topo.die(c) and topo.may_write(k, p)]
        if topo.chip(c) != topo.chip(p) and same.index(c) % 2 and free:
            via[c] = free[0]
    return via


def hand_on(g, core, T, topo, src):
    r = NR - 1
    dst = T.cores[T.rank_of(src) ^ MASKS[r]]
    lo, hi = HP[0]
    rid, pid, _ = topo.addr(dst)
    for k, piece in enumerate((T["hl%d" % r][:, lo:hi].bitcast(dt.uint8), T["hls%d" % r][:, lo:hi])):
        g.wait_ge(T.sem["hand%d" % k], len(topo.engines(src, core)))
        g.remote_dma(piece, piece, T.sem["a_h%d_0" % r], T.sem["loc"], pid, rid, topo.mask(core, dst))
    g.wait_ge(T.sem["loc"], 2 * len(topo.engines(core, dst)))


def rank_program(g, core, T, topo):
    rank = T.rank_of(core)
    via = helpers(T, topo)
    if rank is None:
        for src, k in via.items():
            if k == core:
                hand_on(g, core, T, topo, src)
        return
    que = {"v": g.vector, "s": g.scalar, "t": g.tensor, "g": g, "y": g.sync}
    total, know, recs = {}, {}, {}
    clk = {e: {} for e in que}

    def a(name, idx=None):
        shape = SCRATCH[name][1]
        idx = s_[:] if idx is None else idx
        at = np.arange(int(np.prod(shape[1:]))).reshape([1] + shape[1:])[(slice(None),) + (idx[1:] if isinstance(idx, tuple) else ())]
        m = np.zeros(int(np.prod(shape[1:])), bool)
        m[at.reshape(-1)] = True
        if name == "pb":
            m = np.repeat(m.reshape(8, 512).any(axis=1), 512)
        return (T[name][idx], [(name, m)])

    def cols(name, lo, hi):
        return a(name, s_[:, lo:hi])

    def by(win, off):
        return (win[0].indirect(off[0]), win[1] + off[1])

    def raw(x, kind):
        return (x[0].bitcast(kind), x[1])

    def hbm(ap):
        return (ap, [])

    def need(e, ev):
        sem, val = ev
        c = clk[e]
        if c.get(sem, 0) >= val:
            return
        que[e].wait_ge(T.sem[sem], val)
        c[sem] = val
        for k, w in know.get(ev, {}).items():
            if c.get(k, 0) < w:
                c[k] = w

    def hazards(e, rd, wr):
        best = {}
        for w, regs in ((False, rd), (True, wr)):
            for n, m in regs:
                for (m2, w2, ev, e2) in recs.get(n, ()):
                    if (w or w2 or (n == "pb" and e2 != e)) and (m & m2).any():
                        best[ev[0]] = max(best.get(ev[0], 0), ev[1])
        for s in sorted(best, key=lambda k: -best[k]):
            need(e, (s, best[s]))

    def note(e, rd, wr, ev):
        for n, m in wr:
            recs[n] = [x for x in recs.get(n, []) if (x[0] & ~m).any()] + [(m, True, ev, e)]
        for n, m in rd:
            recs[n] = [x for x in recs.get(n, []) if x[1] or x[2][0] != ev[0] or (x[0] & ~m).any()] + [(m, False, ev, e)]

    def issue(e, sem, step, fn, ins, outs):
        rd = [r for x in ins if isinstance(x, tuple) for r in x[1]]
        wr = [r for x in outs for r in x[1][:1]]
        rd += [r for x in outs for r in x[1][1:]]
        hazards(e, rd, wr)
        total[sem] = total.get(sem, 0) + step
        ev = (sem, total[sem])
        know[ev] = dict(clk[e])
        fn(que[e]).then_inc(T.sem[sem], step)
        note(e, rd, wr, ev)

    def op(e, fn, ins, outs):
        if e == "g" and "cg" in total:
            need("g", ("cg", total["cg"]))
        issue(e, "c" + e, 1, fn, ins, outs)

    def dma(e, sem, out, in_):
        issue(e, sem, 16, lambda q: q.dma_start(out[0], in_[0]), [in_], [out])

    def send(dst, sem, out, in_):
        hazards("g", in_[1], [])
        rid, pid, _ = topo.addr(dst)
        g.remote_dma(out[0], in_[0], T.sem[sem], T.sem["loc"], pid, rid, topo.mask(core, dst))
        total["loc"] = total.get("loc", 0) + len(topo.engines(core, dst))

    def lands(src, sem, what):
        total[sem] = len(what) * len(topo.engines(src, core))
        for x in what:
            for n, m in x[1]:
                recs.setdefault(n, []).append((m, True, (sem, total[sem]), "remote"))

    part = [T.cores[rank ^ m] for m in MASKS]
    for r in range(NR):
        lands(part[r], "a_sc%d" % r, [a("tc%d" % r)])
        lands(part[r], "a_le%d" % r, [a("le%d" % r)])
        lands(part[r], "a_lm%d" % r, [a("lm%d" % r)])
        for i, (lo, hi) in enumerate(HP):
            src = via.get(part[r], part[r]) if (r, i) == (NR - 1, 0) else part[r]
            lands(src, "a_h%d_%d" % (r, i), [cols("hl%d" % r, lo, hi), cols("hls%d" % r, lo, hi)])

    def val(x):
        return x[0] if isinstance(x, tuple) else x

    def ts(out, in0, s1, o0, s2=None, o1=None):
        if o1 is None:
            op("v", lambda q: q.tensor_scalar(out[0], in0[0], val(s1), None, o0), [in0, s1], [out])
        else:
            op("v", lambda q: q.tensor_scalar(out[0], in0[0], val(s1), val(s2), o0, o1), [in0, s1, s2], [out])

    def tt(out, x, y, o):
        op("v", lambda q: q.tensor_tensor(out[0], x[0], y[0], o), [x, y], [out])

    def cp(out, in_):
        op("v", lambda q: q.tensor_copy(out[0], in_[0]), [in_], [out])

    def fill(out, c):
        op("v", lambda q: q.memset(out[0], c), [], [out])

    def turn(out, in_):
        op("v", lambda q: q.transpose(out[0], in_[0]), [in_], [out])

    def scan(out, d0, d1, o):
        op("v", lambda q: q.tensor_tensor_scan(out[0], d0[0], d1[0], 0.0, A.mult, o), [d0, d1], [out])

    def act(out, in_, scale=None, bias=None):
        if bias is not None:
            op("s", lambda q: q.activation(out[0], in_[0], F.Identity, bias=val(bias), scale=1.0 if scale is None else scale), [in_, bias], [out])
        elif scale is not None:
            op("s", lambda q: q.activation(out[0], in_[0], F.Copy, scale=scale), [in_], [out])
        else:
            op("s", lambda q: q.activation(out[0], in_[0], F.Copy), [in_], [out])

    def move(e, out, in_, scale=None):
        if e == "s":
            act(out, in_, scale)
        elif scale is None:
            cp(out, in_)
        else:
            ts(out, in_, scale, A.mult)

    def quant(name, lo, hi, in_):
        q_, p_ = cols(name[0], lo, hi), cols(name[1], lo, hi)
        op("v", lambda q: q.quantize_mx(q_[0], p_[0], in_[0]), [in_], [q_, p_])

    def bank(k, lo, hi):
        return cols("pb", 512 * k + lo, 512 * k + hi)

    def mm(k, left, l0, right, lo, hi):
        x = [cols(left[0], l0, l0 + 128), cols(left[1], l0, l0 + 128), cols(right[0], lo, hi), cols(right[1], lo, hi)]
        out = bank(k, 0, hi - lo)
        op("t", lambda q: q.matmul_mx(out[0], x[0][0], x[1][0], x[2][0], x[3][0], True, True), x, [out])

    def iota(out, pattern, base, cm, fl=False):
        if fl:
            op("g", lambda q: q.iota(out[0], pattern, base, cm, allow_small_or_imprecise_dtypes=True), [], [out])
        else:
            op("g", lambda q: q.iota(out[0], pattern, base, cm), [], [out])

    def row(name, lo, hi=None, step=1):
        at = lo if hi is None else slice(lo, hi, step)
        return a(name, s_[:, 0:12, :, at] if name == "kt" else s_[:, :, at])

    def blocks(name, lo, hi):
        return a(name, s_[:, lo // 32:hi // 32] if name == "kt" else s_[:, lo // 16:hi // 16, :])

    def offs(name, lo, hi):
        return cols(name, lo // 16, hi // 16)

    def swap1(mid, src):
        for h in range(2):
            turn(a(mid, s_[:, :, h, :]), src(h))

    def swap2(dst, mid):
        for m in range(2):
            turn(dst(m), a(mid, s_[:, m::2, :, :]))

    UQ, UR, VQ, WQ, EQ, XQ, ZQ, ZO = [(n, n + "s") for n in ("uq", "ur", "vq", "wq", "eq", "xq", "zq", "zo")]
    fbias, vbias = cols("ct", 0, 1), cols("ct", 32, 33)

    dma("y", "ld_dl", a("dli"), hbm(T.dl[:]))
    dma("s", "ld_u", a("u0"), hbm(T.u[:]))
    for i, (lo, hi) in enumerate(SP):
        dma("ys"[i], "ld_x%d" % i, cols("x0", 4 * lo, 4 * hi), hbm(T.x[:, 4 * lo:4 * hi]))
    need("y", ("ld_x0", 16))
    dma("y", "ld_nl", a("nli"), hbm(T.nl[:]))
    dma("y", "ld_wc", raw(a("wq"), dt.uint8), hbm(T.wc[:]))
    dma("y", "ld_wsp", a("wqs"), hbm(T.ws[:]))
    dma("y", "ld_v", a("v0"), hbm(T.v[:]))

    fill(a("ones"), 1.0)
    for k in range(4):
        iota(a("cT", s_[32 * k:32 * k + 32, :]), [[32, 12], [0, 2]], 0, 1, True)
    iota(a("iu"), [[16, 8]], 0, 0)
    iota(a("iota"), [[1, C]], -int(MID), 0, True)
    op("g", lambda q: q.affine_select(T.dg[:], T.ones[:], [[-1, 516]], A.is_equal, 0.0, 3, 4), [a("ones")], [a("dg")])
    for name, c in (("k1", HUGE), ("ko", HUGE), ("kp", 0.0)):
        act(a(name), cols("ones", 0, C), c)
    fill(a("vt"), HUGE)
    fill(a("vt", s_[:, 0, :, 4:7]), 0.0)
    fill(a("vt", s_[:, 0, :, 12:15]), -BIG * ONE)
    fill(a("vt", s_[:, 1, :, 1:8]), 0.0)
    fill(row("kt", 0, 16, 15), HUGE)
    fill(cols("sa", 336, 448), 0.0)
    fill(a("new"), 0.0)
    fill(a("fl"), 0.0)
    fill(a("kt", s_[:, 12:16, :, 10:12]), 0.0)
    turn(a("ct"), a("vt"))
    for name, runs, places in (("k1", ((2, 4), (5, 8)), ((9, 1024.0), (12, 4096.0 + BIG))), ("ko", ((3, 4), (6, 8)), ((10, 2048.0), (13, 5120.0 + BIG)))):
        for lo, hi in runs:
            fill(row(name, lo, hi), -HUGE)
        for r_, k in places:
            ts(row(name, r_), a("cT"), k, A.add, ONE, A.mult)
        if name == "k1":
            turn(a("tw1"), a("k1"))
    ts(row("kt", 8), a("cT"), ONE, A.mult)
    cp(a("lu"), a("iu"))
    ts(row("kp", 3), a("cT"), -MID, A.add)
    ts(row("dd", 6), a("cT"), 1024.0, A.add, ONE, A.mult)

    def newv(k):
        return a("new", s_[:, 0:12, :, k])

    def own_tables():
        act(row("ko", 11), newv(0), ONE, (MID + 3072.0) * ONE)
        act(row("ko", 14), newv(0), ONE, (MID + 6144.0 + BIG) * ONE)

    def send_d(r):
        send(part[r], "a_le%d" % r, a("le%d" % r), a("ld%d" % r))

    def places_for_partner(r):
        act(a("rl"), by(a("ri"), a("le%d" % r)))

    def score(xn, i):
        lo, hi = SP[i]
        quant(XQ, lo, hi, cols(xn, 4 * lo, 4 * hi))
        mm(i, UR, 0, XQ, lo, hi)

    cp(a("ld0"), a("dli"))
    send_d(0)
    ts(a("fl", s_[:, 0:12, :]), a("dli"), -MID, A.add)
    quant(UQ, 0, 128, a("u0"))
    swap1("r4a", lambda h: a("fl", s_[:, :, h]))
    cp(raw(a("ur"), dt.uint32), by(raw(a("uq"), dt.uint32), a("lu")))
    act(a("urs"), by(a("uqs"), a("lu")))
    swap2(lambda m: a("ol", s_[:, :, m]), "r4a")
    cp(newv(0), a("ol", s_[:, 0:12, :]))
    own_tables()
    act(row("kp", 1), newv(0))
    cp(by(a("ri"), a("ld0")), a("iota"))
    score("x0", 0)
    turn(a("tw0"), a("ko"))
    score("x0", 1)

    state = ["x0", "xa1", "xa2", "xa1"]
    for r in range(NR):
        p = part[r]
        xn, xm = state[r], state[r + 1]
        ld, tc, sc = a("ld%d" % r), "tc%d" % r, "sc%d" % r
        l3, m3 = a("l3%d" % r), a("m3%d" % r)
        more = r + 1 < NR

        def halve(t):
            act(cols("hx", C * t, C * t + C), a(xn, s_[:, t:4 * C:4]), 0.5)

        def send_places():
            act(a("ls%d" % r), row("tl", 0))
            send(p, "a_lm%d" % r, a("lm%d" % r), a("ls%d" % r))

        for i, (lo, hi) in enumerate(SP):
            tt(cols("v0t", lo, hi), bank(i, 0, hi - lo), cols("tw0", lo, hi), A.max)
            tt(cols("v1t", lo, hi), bank(i, 0, hi - lo), cols("tw1", lo, hi), A.max)
            act(cols("v2t", lo, hi), bank(i, 0, hi - lo), bias=vbias)
        tt(a("w1"), by(a("v0t"), ld), a("v1t"), A.min)
        halve(0)
        tt(a("w2"), by(a("w1"), ld), a("v2t"), A.min)
        turn(a("po2"), a("w2"))
        act(a("fo"), a("w2"), bias=fbias)
        cp(row(sc, 3, 5), row("po2", 10, 12))
        cp(row(sc, 0, 3), row("po2", 1, 4))
        send(p, "a_sc%d" % r, a(tc), a(sc))
        if r == 0:
            places_for_partner(0)
        halve(1)
        ts(a("fl", s_[:, 0:12, :]), row("po2", 11), 1.0 / ONE, A.mult, -3072.0, A.add)
        cp(a("fl", s_[:, 12:24, :]), a("le%d" % r))
        swap1("r4a", lambda h: a("fl", s_[:, :, h]))
        if r:
            turn(a("tl"), a("rl"))
        swap2(lambda m: a("ol", s_[:, :, m]), "r4a")
        cp(l3, a("ol", s_[:, 0:12, :]))
        if r:
            send_places()
        act(row("kt", 9), a("ol", s_[:, 12:24, :]), ONE, 1024.0 * ONE)
        act(row("kt", 12), a("ol", s_[:, 12:24, :]), ONE, (4096.0 + BIG) * ONE)
        tt(a("w1"), by(a("fo"), l3), a("w2"), A.min)
        halve(2)
        halve(3)
        if r == 0:
            turn(a("tl"), a("rl"))
            send_places()
            cp(a("ln"), a("nli"))
        turn(a("po3"), a("w1"))
        ts(row("po3", 8), a("cT"), ONE, A.mult)
        tt(row("po3", 4, 6), row("po3", 4, 6), row("po3", 3, 8, 4), A.min)
        tt(row("dd", 0, 6), row("po3", 14, 8, -1), row("po3", 13, 7, -1), A.subtract)
        if more:
            turn(a("ti"), a("ri"))
            cp(newv(3), row("ti", 0))
        act(row("kt", 4, 7), row(tc, 0, 3))
        cp(row("kt", 10, 12), row(tc, 3, 5))
        cp(row("kt", 1, 4), row(tc, 0, 3))
        cp(row("kt", 7), row(tc, 2))
        ts(row("kt", 13, 15), row(tc, 3, 5), (3072.0 + BIG) * ONE, A.add)
        swap1("r4a", lambda h: a("kt", s_[:, :, h, 10:12]))
        for lo, hi in HALF:
            turn(cols("wt", lo, hi), blocks("kt", lo, hi))
            if lo == 0:
                act(cols("ft", lo, hi), cols("wt", lo, hi), bias=fbias)
                swap2(lambda m: a("oe", s_[:, :, :, m]), "r4a")
        ts(m3, a("oe", s_[:, 0:12, 1, :]), 1.0 / ONE, A.mult, -3072.0, A.add)
        ts(cols("ft", 192, C), cols("wt", 192, C), fbias, A.add)
        tt(a("wu"), by(a("ft"), m3), a("wt"), A.min)
        act(a("da"), a("dd"), 1.0 / ONE, -1024.0)
        for e, (lo, hi) in zip("vs", HALF):
            move(e, cols("vv", lo, hi), by(a("wu"), offs("ln", lo, hi)))
        for lo, hi in HALF:
            turn(blocks("pt", lo, hi), cols("vv", lo, hi))
        tt(row("pt", 4, 6), row("pt", 4, 6), row("pt", 3, 8, 4), A.min)
        act(a("db"), row("pt", 8, 15), -1.0 / ONE, 8191.0)
        tt(a("c8"), row("po3", 7, 0, -1), row("pt", 0, 7), A.is_gt)
        scan(cols("sa", 0, 168), a("c8"), a("da"), A.add)
        scan(cols("sa", 168, 336), a("c8"), a("db"), A.max)
        swap1("r4b", lambda h: a("sa", s_[:, 7 * h + 6:448:14]))
        cp(cols("nk", 0, 24), a("sa", s_[:, 174:336:7]))
        swap2(lambda m: a("oa", s_[:, :, m]), "r4b")
        cp(a("la"), a("oa", s_[:, 0:12, :]))
        cp(a("ni"), a("oa", s_[:, 12:24, :]))
        ts(cols("nk", 24, 48), cols("nk", 0, 24), 10, A.logical_shift_right, 1, A.bitwise_and)
        ts(a("nj"), a("ni"), 1023, A.bitwise_and)
        cp(row("kp", 4), cols("nk", 24, 48))
        ts(a("lb"), a("nj"), -1.0, A.mult, 1023.0, A.add)
        cp(row("kp", 2), a("lm%d" % r))
        turn(a("rk"), a("kp"))

        def half_a(lo, hi):
            for t in range(4):
                act(cols("za", C * t + lo, C * t + hi), by(cols("hx", C * t, C * t + C), offs("la", lo, hi)))

        def half_b(lo, hi):
            for t in range(4):
                tt(a("zt", s_[:, 4 * lo + t:4 * hi:4]), by(cols("hx", C * t, C * t + C), offs("lb", lo, hi)), cols("za", C * t + lo, C * t + hi), A.add)

        HQ, HL = ("hq%d" % r, "hqs%d" % r), ("hl%d" % r, "hls%d" % r)

        def layer(i):
            lo, hi = HP[i]
            quant(ZQ, lo, hi, cols("zt", 4 * lo, 4 * hi))
            for k in range(4):
                mm(4 * i + k, WQ, 128 * k, ZQ, lo, hi)

        def hcopy(i, who):
            lo, hi = HP[i]
            for k, e in enumerate(who):
                move(e, a("ht", s_[:, 4 * lo + k:4 * hi:4]), bank(4 * i + k, 0, hi - lo), 0.03125)

        def hsend(i):
            lo, hi = HP[i]
            quant(HQ, lo, hi, cols("ht", 4 * lo, 4 * hi))
            around = i == 0 and not more and core in via
            to, sems = (via[core], ("hand0", "hand1")) if around else (p, ("a_h%d_%d" % (r, i),) * 2)
            send(to, sems[0], raw(cols(HL[0], lo, hi), dt.uint8), raw(cols(HQ[0], lo, hi), dt.uint8))
            send(to, sems[1], cols(HL[1], lo, hi), cols(HQ[1], lo, hi))

        half_a(*HP[0])
        half_a(*HP[1])
        half_b(*HP[0])
        layer(0)
        half_b(*HP[1])
        layer(1)
        hcopy(0, "sssv")
        hsend(0)
        hcopy(1, "vsvv")
        half_a(FAR, C)
        act(a("rn"), by(a("rk"), a("ln")))
        hsend(1)
        half_b(FAR, C)
        quant(ZO, 0, 128, cols("zt", 4 * (C - 128), 4 * C))
        for k in range(4):
            mm(k, WQ, 128 * k, ZO, 0, 128)
        if r == 0:
            for b in range(4):
                quant(EQ, 128 * b, 128 * b + 128, cols("dg", 3 - b, 515 - b))

        def own_columns(k):
            move("v", cols("jt", C * k + FAR, C * k + C), bank(k, 128 - (C - FAR), 128), 0.03125)

        kinds = 3 if more else 2
        turn(a("kn"), a("rn"))
        own_columns(0)
        tt(a("odd"), row("kp", 4), row("kn", 4), A.not_equal)
        tt(row("dlt", 0, kinds), row("kn", 1, 1 + kinds), row("kp", 1, 1 + kinds), A.subtract)
        own_columns(1)
        for k in range(kinds):
            tt(row("prd", k), a("odd"), row("dlt", k), A.mult)
        own_columns(2)
        tt(a("new", s_[:, 0:12, :, 0:kinds]), row("prd", 0, kinds), row("kp", 1, 1 + kinds), A.add)
        own_columns(3)
        swap1("r5", lambda h: a("new", s_[:, :, h, :]))
        if more:
            own_tables()
            act(row("ko", 0), newv(2))
            cp(row("kp", 1), newv(0))
        swap2(lambda m: a("ob", s_[:, :, :, m]), "r5")
        nl_ = "ld%d" % (r + 1) if more else "ldf"
        ts(a(nl_), a("ob", s_[:, 0:12, 0, :]), MID, A.add)
        ts(a("ll"), a("ob", s_[:, 0:12, 1, :]), MID, A.add)
        if more:
            send_d(r + 1)
            ts(a("li"), a("ob", s_[:, 0:12, 3, :]), MID, A.add)
            turn(a("tw0"), a("ko"))
        else:
            quant(VQ, 0, 128, a("v0"))
            act(a("v0t"), by(a("iota"), a("ldf")), bias=MID)
            dma("y", "out", hbm(T.dn[:]), a("v0t", s_[0:128:16, :]))

        def unpack(i, b0, who):
            lo, hi = HP[i]
            for k in range(4):
                mm(b0 + k, EQ, 128 * k, HL, lo, hi)
            for k, e in enumerate(who):
                move(e, cols("jt", C * k + lo, C * k + hi), bank(b0 + k, 0, hi - lo))

        late = 0 if not more and p in via else 1
        unpack(1 - late, 4, "ssss" if more else "vsvs")
        unpack(late, 0, "vsss")
        lo, hi = SP[1]
        for t in range(4):
            act(a("jg", s_[:, t:4 * (hi - lo):4]), by(cols("jt", C * t, C * t + C), offs("ll", lo, hi)))
        if more:
            act(a("ri"), by(a("tw0"), a("li")))
            places_for_partner(r + 1)
        for i, (lo, hi) in enumerate(SP):
            if i == 0:
                for t in range(4):
                    tt(a(xm, s_[:, 4 * lo + t:4 * hi:4]), by(cols("jt", C * t, C * t + C), offs("ll", lo, hi)), a(xn, s_[:, 4 * lo + t:4 * hi:4]), A.add)
            else:
                tt(cols(xm, 4 * lo, 4 * hi), a("jg"), cols(xn, 4 * lo, 4 * hi), A.add)
            if more:
                score(xm, i)
            else:
                quant(XQ, lo, hi, cols(xm, 4 * lo, 4 * hi))
                mm(4 + i, VQ, 0, XQ, lo, hi)
                dma("y", "out", hbm(T.oc[:, 4 * lo:4 * hi]), raw(cols("xq", lo, hi), dt.uint8))
                if i:
                    for k in range(4):
                        dma("ys"[k % 2], "out", hbm(T.osc[4 * k:4 * k + 4, :]), a("xqs", s_[32 * k:32 * k + 4, :]))
                move("sv"[i], cols("ysb", lo, hi), bank(4 + i, 0, hi - lo))
                dma("s", "out", hbm(T.y[:, lo:hi]), cols("ysb", lo, hi))
    for s, v in total.items():
        need("g", (s, v))
